import numpy as np
import ml_dtypes


def mxq(x, axis, fmt="e4m3"):
    dtype, down = {"e4m3": (ml_dtypes.float8_e4m3fn, 7), "e5m2": (ml_dtypes.float8_e5m2, 14)}[fmt]
    v = np.moveaxis(np.asarray(x, np.float32).astype(ml_dtypes.bfloat16).astype(np.float64), axis, -1)
    blocks = v.reshape(v.shape[:-1] + (-1, 32))
    amax = np.abs(blocks).max(-1, keepdims=True)
    byte = np.maximum(np.where(amax > 0, np.frexp(amax)[1] - 1 + 127, 0) - down, 1)
    scale = np.exp2(byte - 127.0)
    codes = (blocks / scale).astype(np.float32).astype(dtype).astype(np.float64)
    return np.moveaxis((codes * scale).reshape(v.shape), -1, axis)


WIDE = False


def mx_kscale(k):
    if not WIDE:
        return np.ones(k)
    levels = np.array([10, -10, 5, -5, 0])
    if k % 512:
        return np.exp2(np.random.permutation(np.resize(levels, k // 32))).repeat(32)
    a = np.empty((k // 512, 16))
    for p in range(k // 512):
        a[p, :8] = np.random.permutation(np.resize(levels, 8))
        for g in range(8):
            far = levels[np.abs(levels - a[p, g]) >= 10]
            a[p, g + 8] = far[np.random.randint(len(far))]
    return np.exp2(a.ravel()).repeat(32)


def f64(x):
    return np.asarray(x).astype(np.float64)


def striped(idx):
    return np.tile(idx.reshape(-1, 16).T, (8, 1)).astype(np.uint16)


def unstriped(offs):
    return offs[:16].T.reshape(-1).astype(np.int64)


def pack_weight(w):
    k, n = w.shape
    w = f64(np.asarray(w, np.float32).astype(ml_dtypes.bfloat16)).reshape(k // 32, 32, n)
    amax = np.abs(w).max(1)
    byte = np.clip(np.where(amax > 0, np.frexp(amax)[1] - 1 + 127 - 7, 1), 1, 254)
    scaled = (w * np.exp2(127.0 - byte)[:, None, :]).reshape(k, n).astype(np.float32)
    words = np.ascontiguousarray(scaled.reshape(k // 512, 128, 4, n).transpose(0, 1, 3, 2)).astype(ml_dtypes.float8_e4m3fn).view(np.uint8)
    return words, np.ascontiguousarray(byte.astype(np.uint8).reshape(k // 512, 16, n))


def unpack_weight(words, scales):
    g, p, n, _ = words.shape
    vals = np.ascontiguousarray(words).view(ml_dtypes.float8_e4m3fn).astype(np.float64) * np.repeat(np.exp2(scales.astype(np.float64) - 127.0), 8, axis=1)[..., None]
    return vals.transpose(0, 1, 3, 2).reshape(g * 512, n)


K, T, H, N = 1024, 512, 512, 256


def setup_inputs():
    n = np.random.standard_normal
    s = mx_kscale(K)[:, None]
    u = mx_kscale(H)
    packed_xT = pack_weight(n((K, T)) * s)
    return {
        "x_words": packed_xT[0],
        "x_scales": packed_xT[1],
        "w1": (n((K, H)) / np.sqrt(K) / s * u).astype(np.float32),
        "w2": (n((H, N)) / np.sqrt(3 * H) / u[:, None]).astype(np.float32),
        "w3": (n((H, N)) / np.sqrt(3 * H) / u[:, None]).astype(np.float32),
        "w4": (n((H, N)) / np.sqrt(3 * H) / u[:, None]).astype(np.float32),
        "pos1": striped(np.random.permutation(T)),
        "pos2": striped(np.random.permutation(T)),
        "pos3": striped(np.random.permutation(T)),
        "pos4": striped(np.random.permutation(T)),
    }


def reference(x_words, x_scales, w1, w2, w3, w4, pos1, pos2, pos3, pos4):
    xq = unpack_weight(x_words, x_scales)
    h = mxq(f64(w1), 0, "e4m3").T @ xq
    g0 = h[:, unstriped(pos1)]
    g1 = h[:, unstriped(pos2)]
    g2 = h[:, unstriped(pos3)]
    g3 = h[:, unstriped(pos4)]
    z1 = (g0 + g1 + g2 + g3) / 4
    z2 = np.maximum(np.maximum(np.maximum(g0, g1), g2), g3)
    z3 = np.minimum(np.minimum(np.minimum(g0, g1), g2), g3)
    return mxq(f64(w2), 0, "e4m3").T @ mxq(z1, 0, "e4m3") + mxq(f64(w3), 0, "e4m3").T @ mxq(z2, 0, "e4m3") + mxq(f64(w4), 0, "e4m3").T @ mxq(z3, 0, "e4m3")

@@ -1,0 +1,202 @@
+from contextlib import ExitStack
+
+import concourse.mybir as mybir
+from concourse.masks import make_identity
+
+K, T, H, N = 1024, 512, 512, 256
+FLOPS = 2 * K * H * T + 3 * 2 * H * N * T
+
+F32 = mybir.dt.float32
+BF16 = mybir.dt.bfloat16
+I32 = mybir.dt.int32
+U32 = mybir.dt.uint32
+U16 = mybir.dt.uint16
+U8 = mybir.dt.uint8
+FP8X4 = mybir.dt.float8_e4m3fn_x4
+COPY = mybir.ActivationFunctionType.Copy
+MAX = mybir.AluOpType.max
+MIN = mybir.AluOpType.min
+
+P = 128
+PACK = 4
+D = 4
+CHUNK = 256
+CHUNKS = T // CHUNK
+BLOCKS = CHUNK // P
+
+
+def tile_picked_wpna_none_l_kernel(
+    tc, x_words, x_scales, w1, w2, w3, w4, pos1, pos2, pos3, pos4, out
+):
+    nc = tc.nc
+    with ExitStack() as ctx:
+        keep = ctx.enter_context(tc.tile_pool(name="keep", bufs=1))
+        psum_a = ctx.enter_context(tc.psum_pool(name="psum_a", bufs=4))
+        psum_b = ctx.enter_context(tc.psum_pool(name="psum_b", bufs=4))
+
+        lists = [keep.tile([P, T // 16], U16, name="list%d" % d) for d in range(D)]
+        x_codes = [keep.tile([P, T], U32, name="x_codes%d" % z, align_bytes=64) for z in range(2)]
+        x_plane = keep.tile([P, 2, T], U8, name="x_plane", align_bytes=64)
+        nc.vector.memset(x_plane[:].bitcast(I32), 0)
+
+        def load_x(z):
+            nc.sync.dma_start(x_codes[z][:].bitcast(I32), x_words[z].rearrange("p n t -> p (n t)").bitcast(I32))
+
+        def load_w1(z, c0, c1):
+            raw = keep.tile([P, PACK, c1 - c0], F32, name="w1_raw%d_%d" % (z, c0))
+            rows = w1[512 * z : 512 * (z + 1), :].rearrange("(p j) c -> p j c", j=PACK)
+            nc.sync.dma_start(raw[:], rows[:, :, c0:c1])
+            return raw
+
+        w1_raw = {}
+        w1_raw[0, 0] = load_w1(0, 0, 512)
+        load_x(0)
+        scale_rows = x_scales.rearrange("z (q r) n -> q r z n", r=4)
+        for q in range(4):
+            nc.sync.dma_start(x_plane[32 * q : 32 * q + 4, :, :].bitcast(I32), scale_rows[q].bitcast(I32))
+        w1_raw[1, 0] = load_w1(1, 0, 256)
+        w1_raw[1, 256] = load_w1(1, 256, 512)
+        nc.sync.dma_start(lists[0][:], pos1)
+        load_x(1)
+        nc.sync.dma_start(lists[1][:], pos2)
+        nc.sync.dma_start(lists[2][:], pos3)
+        nc.sync.dma_start(lists[3][:], pos4)
+        w_raw = []
+        for s, w in enumerate((w2, w3, w4)):
+            raw = keep.tile([P, PACK, N], F32, name="w_raw%d" % s)
+            nc.sync.dma_start(raw[:], w.rearrange("(p j) n -> p j n", j=PACK))
+            w_raw.append(raw)
+
+        identity = keep.tile([P, P], F32, name="identity")
+        make_identity(nc, identity[:])
+
+        w1_bf = [keep.tile([P, PACK, P, PACK], BF16, name="w1_bf%d" % z, align_bytes=64) for z in range(2)]
+        w1_codes = [keep.tile([P, PACK, P], U32, name="w1_codes%d" % z, align_bytes=64) for z in range(2)]
+        w1_plane = [keep.tile([P, PACK, P], U8, name="w1_plane%d" % z, align_bytes=64) for z in range(2)]
+
+        def cast_w1(z, c0, c1):
+            raw = w1_raw[z, c0]
+            ms = (c1 - c0) // PACK
+            split = (ms * 11 // 16) // 2 * 2
+            src = raw[:].rearrange("p j (m t) -> p m j t", t=PACK)
+            dst = w1_bf[z][:, :, c0 // PACK : c1 // PACK, :].rearrange("p t m j -> p m j t")
+            nc.vector.tensor_copy(dst[:, :split], src[:, :split])
+            nc.scalar.activation(dst[:, split:], src[:, split:], COPY)
+
+        def quantize_w1(z, t0, t1):
+            nc.vector.quantize_mx(
+                out=w1_codes[z][:, t0:t1, :].rearrange("p t m -> p (t m)").bitcast(FP8X4),
+                scales=w1_plane[z][:, t0:t1, :].rearrange("p t m -> p (t m)"),
+                in_=w1_bf[z][:, t0:t1].rearrange("p t m j -> p (t m j)"),
+            )
+
+        cast_w1(0, 0, 512)
+        quantize_w1(0, 0, 4)
+        cast_w1(1, 0, 256)
+        cast_w1(1, 256, 512)
+        for t in range(PACK):
+            quantize_w1(1, t, t + 1)
+
+        h_acc = [psum_a.tile([P, T], F32, name="bank_a", tag="bank_a") for t in range(PACK)]
+        h = [keep.tile([P, T], F32, name="h%d" % t) for t in range(PACK)]
+        for z in range(2):
+            for t in range(PACK):
+                nc.tensor.matmul_mx(
+                    h_acc[t][:],
+                    lhsT=w1_codes[z][:, t, :].bitcast(FP8X4),
+                    lhsT_scale=w1_plane[z][:, t, :],
+                    rhs=x_codes[z][:].bitcast(FP8X4),
+                    rhs_scale=x_plane[:, z, :],
+                    start=(z == 0),
+                    stop=(z == 1),
+                )
+        for t in range(PACK):
+            nc.scalar.copy(h[t][:], h_acc[t][:])
+
+        w_codes, w_plane = [], []
+        for s in range(3):
+            bf = keep.tile([P, N, PACK], BF16, name="w_bf%d" % s, align_bytes=64)
+            nc.scalar.copy(
+                bf[:].rearrange("p (c i) j -> p c j i", i=4),
+                w_raw[s][:].rearrange("p j (c i) -> p c j i", i=4),
+            )
+            codes = keep.tile([P, N], U32, name="w_codes%d" % s, align_bytes=64)
+            plane = keep.tile([P, N], U8, name="w_plane%d" % s, align_bytes=64)
+            nc.vector.quantize_mx(out=codes[:].bitcast(FP8X4), scales=plane[:], in_=bf[:].rearrange("p n j -> p (n j)"))
+            w_codes.append(codes)
+            w_plane.append(plane)
+
+        rounded, mean = [], []
+        for c in range(CHUNKS):
+            rounded.append(keep.tile([P, D, CHUNK, PACK], BF16, name="rounded%d" % c, align_bytes=64))
+            picked = []
+            for d in range(D):
+                g = keep.tile([P, PACK, CHUNK], F32, name="picked%d_%d" % (c, d))
+                offsets = lists[d][:, c * CHUNK // 16 : (c + 1) * CHUNK // 16]
+                for t in range(PACK):
+                    nc.vector.tensor_copy(g[:, t, :], h[t][:].indirect(offsets))
+                nc.scalar.copy(
+                    rounded[c][:, d].rearrange("p (c i) t -> p c t i", i=4),
+                    g[:].rearrange("p t (c i) -> p c t i", i=4),
+                )
+                picked.append(g)
+            back = psum_b.tile([P, BLOCKS, 2, P], F32, name="bank_b", tag="bank_b")
+            for b in range(BLOCKS):
+                total = psum_a.tile([P, PACK, P], F32, name="bank_a", tag="bank_a")
+                for t in range(PACK):
+                    for d in range(D):
+                        nc.tensor.matmul(
+                            total[:, t, :],
+                            lhsT=picked[d][:, t, b * P : (b + 1) * P],
+                            rhs=identity[:],
+                            is_transpose=True,
+                            start=(d == 0),
+                            stop=(d == D - 1),
+                        )
+                turned = keep.tile([P, 2, P, 2], BF16, name="turned%d_%d" % (c, b))
+                nc.scalar.activation(
+                    turned[:], total[:].rearrange("v (u e) p -> v u p e", e=2), COPY, scale=1.0 / D
+                )
+                words = turned[:].rearrange("v u p e -> v u (p e)").bitcast(F32)
+                for u in range(2):
+                    nc.tensor.transpose(back[:, b, u, :], words[:, u, :], identity[:])
+            z1 = keep.tile([P, BLOCKS, P, PACK], BF16, name="mean%d" % c, align_bytes=64)
+            nc.scalar.copy(z1[:].bitcast(F32), back[:].rearrange("p b u v -> p b v u"))
+            mean.append(z1)
+
+        for c in range(CHUNKS):
+            width = CHUNK * PACK
+            low = rounded[c][:, 0:2].rearrange("p d v t -> p (d v t)")
+            high = rounded[c][:, 2:4].rearrange("p d v t -> p (d v t)")
+            stats = [mean[c][:].rearrange("p b v t -> p (b v t)")]
+            halves = []
+            for s, op in ((1, MAX), (2, MIN)):
+                pair = keep.tile([P, 2 * width], BF16, name="pair%d_%d" % (c, s))
+                nc.vector.tensor_tensor(pair[:], low, high, op)
+                halves.append(pair)
+            for s, op in ((1, MAX), (2, MIN)):
+                zs = keep.tile([P, width], BF16, name="stat%d_%d" % (c, s), align_bytes=64)
+                nc.vector.tensor_tensor(zs[:], halves[s - 1][:, :width], halves[s - 1][:, width:], op)
+                stats.append(zs[:])
+            acc = [psum_b.tile([P, CHUNK], F32, name="bank_b", tag="bank_b") for m in range(2)]
+            for s in range(3):
+                codes = keep.tile([P, CHUNK], U32, name="z_codes%d_%d" % (c, s), align_bytes=64)
+                plane = keep.tile([P, CHUNK], U8, name="z_plane%d_%d" % (c, s), align_bytes=64)
+                nc.vector.quantize_mx(out=codes[:].bitcast(FP8X4), scales=plane[:], in_=stats[s])
+                for m in range(2):
+                    nc.tensor.matmul_mx(
+                        acc[m][:],
+                        lhsT=w_codes[s][:, m * P : (m + 1) * P].bitcast(FP8X4),
+                        lhsT_scale=w_plane[s][:, m * P : (m + 1) * P],
+                        rhs=codes[:].bitcast(FP8X4),
+                        rhs_scale=plane[:],
+                        start=(s == 0),
+                        stop=(s == 2),
+                    )
+            for m in range(2):
+                result = keep.tile([P, CHUNK], F32, name="result%d_%d" % (c, m))
+                if c == CHUNKS - 1 and m == 1:
+                    nc.vector.tensor_copy(result[:], acc[m][:])
+                else:
+                    nc.scalar.copy(result[:], acc[m][:])
+                nc.sync.dma_start(out[m * P : (m + 1) * P, c * CHUNK : (c + 1) * CHUNK], result[:])

@@ -20,9 +20,8 @@ MIN = mybir.AluOpType.min
 P = 128
 PACK = 4
 D = 4
-CHUNK = 256
-CHUNKS = T // CHUNK
-BLOCKS = CHUNK // P
+WINDOW = 704
+PIECES = ((0, 256), (256, 384), (384, 512))
 
 
 def tile_picked_wpna_none_l_kernel(
@@ -31,16 +30,24 @@ def tile_picked_wpna_none_l_kernel(
     nc = tc.nc
     with ExitStack() as ctx:
         keep = ctx.enter_context(tc.tile_pool(name="keep", bufs=1))
-        psum_a = ctx.enter_context(tc.psum_pool(name="psum_a", bufs=4))
-        psum_b = ctx.enter_context(tc.psum_pool(name="psum_b", bufs=4))
+        psum = ctx.enter_context(tc.psum_pool(name="psum", bufs=1))
+
+        def bank(b, shape):
+            return psum.tile(shape, F32, name="bank%d" % b, tag="bank%d" % b)
 
         lists = [keep.tile([P, T // 16], U16, name="list%d" % d) for d in range(D)]
-        x_codes = [keep.tile([P, T], U32, name="x_codes%d" % z, align_bytes=64) for z in range(2)]
+        x_codes = keep.tile([P, 2, T], U32, name="x_codes", align_bytes=64)
         x_plane = keep.tile([P, 2, T], U8, name="x_plane", align_bytes=64)
-        nc.vector.memset(x_plane[:].bitcast(I32), 0)
+        h = keep.tile([P, (PACK - 1) * T + WINDOW], F32, name="h")
+        nc.gpsimd.memset(x_plane[:].bitcast(I32), 0)
+        nc.gpsimd.memset(h[:, PACK * T :], 0.0)
 
-        def load_x(z):
-            nc.sync.dma_start(x_codes[z][:].bitcast(I32), x_words[z].rearrange("p n t -> p (n t)").bitcast(I32))
+        def plane_start(t):
+            return (PACK - 1 - t) * T
+
+        def load_x(c0, c1):
+            words = x_words.rearrange("z p n t -> p z (n t)")[:, :, PACK * c0 : PACK * c1]
+            nc.sync.dma_start(x_codes[:, :, c0:c1].bitcast(I32), words.bitcast(I32))
 
         def load_w1(z, c0, c1):
             raw = keep.tile([P, PACK, c1 - c0], F32, name="w1_raw%d_%d" % (z, c0))
@@ -50,17 +57,15 @@ def tile_picked_wpna_none_l_kernel(
 
         w1_raw = {}
         w1_raw[0, 0] = load_w1(0, 0, 512)
-        load_x(0)
+        w1_raw[1, 0] = load_w1(1, 0, 256)
         scale_rows = x_scales.rearrange("z (q r) n -> q r z n", r=4)
         for q in range(4):
             nc.sync.dma_start(x_plane[32 * q : 32 * q + 4, :, :].bitcast(I32), scale_rows[q].bitcast(I32))
-        w1_raw[1, 0] = load_w1(1, 0, 256)
         w1_raw[1, 256] = load_w1(1, 256, 512)
-        nc.sync.dma_start(lists[0][:], pos1)
-        load_x(1)
-        nc.sync.dma_start(lists[1][:], pos2)
-        nc.sync.dma_start(lists[2][:], pos3)
-        nc.sync.dma_start(lists[3][:], pos4)
+        load_x(0, 256)
+        load_x(256, 512)
+        for d, pos in enumerate((pos1, pos2, pos3, pos4)):
+            nc.sync.dma_start(lists[d][:], pos)
         w_raw = []
         for s, w in enumerate((w2, w3, w4)):
             raw = keep.tile([P, PACK, N], F32, name="w_raw%d" % s)
@@ -77,7 +82,7 @@ def tile_picked_wpna_none_l_kernel(
         def cast_w1(z, c0, c1):
             raw = w1_raw[z, c0]
             ms = (c1 - c0) // PACK
-            split = (ms * 11 // 16) // 2 * 2
+            split = ms * 3 // 4
             src = raw[:].rearrange("p j (m t) -> p m j t", t=PACK)
             dst = w1_bf[z][:, :, c0 // PACK : c1 // PACK, :].rearrange("p t m j -> p m j t")
             nc.vector.tensor_copy(dst[:, :split], src[:, :split])
@@ -94,24 +99,28 @@ def tile_picked_wpna_none_l_kernel(
         quantize_w1(0, 0, 4)
         cast_w1(1, 0, 256)
         cast_w1(1, 256, 512)
-        for t in range(PACK):
-            quantize_w1(1, t, t + 1)
+        quantize_w1(1, 0, 1)
+        quantize_w1(1, 1, 2)
+        quantize_w1(1, 2, 4)
 
-        h_acc = [psum_a.tile([P, T], F32, name="bank_a", tag="bank_a") for t in range(PACK)]
-        h = [keep.tile([P, T], F32, name="h%d" % t) for t in range(PACK)]
-        for z in range(2):
-            for t in range(PACK):
+        def first_product(b, t, c0, c1, engine_copy):
+            acc = bank(b, [P, c1 - c0])
+            for z in range(2):
                 nc.tensor.matmul_mx(
-                    h_acc[t][:],
+                    acc[:],
                     lhsT=w1_codes[z][:, t, :].bitcast(FP8X4),
                     lhsT_scale=w1_plane[z][:, t, :],
-                    rhs=x_codes[z][:].bitcast(FP8X4),
-                    rhs_scale=x_plane[:, z, :],
+                    rhs=x_codes[:, z, c0:c1].bitcast(FP8X4),
+                    rhs_scale=x_plane[:, z, c0:c1],
                     start=(z == 0),
                     stop=(z == 1),
                 )
-        for t in range(PACK):
-            nc.scalar.copy(h[t][:], h_acc[t][:])
+            engine_copy(h[:, plane_start(t) + c0 : plane_start(t) + c1], acc[:])
+
+        first_product(0, 0, 0, 256, nc.scalar.copy)
+        first_product(1, 0, 256, 512, nc.vector.tensor_copy)
+        for t in range(1, PACK):
+            first_product(1 + t, t, 0, T, nc.scalar.copy)
 
         w_codes, w_plane = [], []
         for s in range(3):
@@ -126,62 +135,78 @@ def tile_picked_wpna_none_l_kernel(
             w_codes.append(codes)
             w_plane.append(plane)
 
-        rounded, mean = [], []
-        for c in range(CHUNKS):
-            rounded.append(keep.tile([P, D, CHUNK, PACK], BF16, name="rounded%d" % c, align_bytes=64))
-            picked = []
-            for d in range(D):
-                g = keep.tile([P, PACK, CHUNK], F32, name="picked%d_%d" % (c, d))
-                offsets = lists[d][:, c * CHUNK // 16 : (c + 1) * CHUNK // 16]
-                for t in range(PACK):
-                    nc.vector.tensor_copy(g[:, t, :], h[t][:].indirect(offsets))
-                nc.scalar.copy(
-                    rounded[c][:, d].rearrange("p (c i) t -> p c t i", i=4),
-                    g[:].rearrange("p t (c i) -> p c t i", i=4),
-                )
-                picked.append(g)
-            back = psum_b.tile([P, BLOCKS, 2, P], F32, name="bank_b", tag="bank_b")
-            for b in range(BLOCKS):
-                total = psum_a.tile([P, PACK, P], F32, name="bank_a", tag="bank_a")
-                for t in range(PACK):
-                    for d in range(D):
-                        nc.tensor.matmul(
-                            total[:, t, :],
-                            lhsT=picked[d][:, t, b * P : (b + 1) * P],
-                            rhs=identity[:],
-                            is_transpose=True,
-                            start=(d == 0),
-                            stop=(d == D - 1),
-                        )
-                turned = keep.tile([P, 2, P, 2], BF16, name="turned%d_%d" % (c, b))
+        totals = [bank(1 + b, [P, PACK, P]) for b in range(T // P)]
+        rounded = [keep.tile([P, T, PACK], BF16, name="rounded%d" % d, align_bytes=64) for d in range(D)]
+
+        def gather(d, v0, v1):
+            g = keep.tile([P, PACK, v1 - v0], F32, name="picked%d_%d" % (d, v0))
+            offsets = lists[d][:, v0 // 16 : v1 // 16]
+            for t in range(PACK):
+                window = h[:, plane_start(t) : plane_start(t) + WINDOW]
+                nc.vector.tensor_copy(g[:, t, :], window.indirect(offsets))
+                for b in range(v0 // P, v1 // P):
+                    nc.tensor.matmul(
+                        totals[b][:, t, :],
+                        lhsT=g[:, t, b * P - v0 : (b + 1) * P - v0],
+                        rhs=identity[:],
+                        is_transpose=True,
+                        start=(d == 0 and t == 0),
+                        stop=(d == D - 1 and t == PACK - 1),
+                    )
+            nc.scalar.copy(
+                rounded[d][:, v0:v1].rearrange("p (c i) t -> p c t i", i=4),
+                g[:].rearrange("p t (c i) -> p c t i", i=4),
+            )
+
+        mean = keep.tile([P, T, PACK], BF16, name="mean", align_bytes=64)
+
+        def finish_mean(v0, v1, b_back):
+            blocks = (v1 - v0) // P
+            back = bank(b_back, [P, blocks, 2, P])
+            for i in range(blocks):
+                b = v0 // P + i
+                turned = keep.tile([P, 2, P, 2], BF16, name="turned%d" % b)
                 nc.scalar.activation(
-                    turned[:], total[:].rearrange("v (u e) p -> v u p e", e=2), COPY, scale=1.0 / D
+                    turned[:], totals[b][:].rearrange("v (u e) p -> v u p e", e=2), COPY, scale=1.0 / D
                 )
                 words = turned[:].rearrange("v u p e -> v u (p e)").bitcast(F32)
                 for u in range(2):
-                    nc.tensor.transpose(back[:, b, u, :], words[:, u, :], identity[:])
-            z1 = keep.tile([P, BLOCKS, P, PACK], BF16, name="mean%d" % c, align_bytes=64)
-            nc.scalar.copy(z1[:].bitcast(F32), back[:].rearrange("p b u v -> p b v u"))
-            mean.append(z1)
+                    nc.tensor.transpose(back[:, i, u, :], words[:, u, :], identity[:])
+            nc.scalar.copy(
+                mean[:, v0:v1].bitcast(F32).rearrange("p (b v) u -> p b v u", b=blocks),
+                back[:].rearrange("p b u v -> p b v u"),
+            )
 
-        for c in range(CHUNKS):
-            width = CHUNK * PACK
-            low = rounded[c][:, 0:2].rearrange("p d v t -> p (d v t)")
-            high = rounded[c][:, 2:4].rearrange("p d v t -> p (d v t)")
-            stats = [mean[c][:].rearrange("p b v t -> p (b v t)")]
-            halves = []
+        for d in range(D - 1):
+            gather(d, 0, T)
+        gather(D - 1, 0, 256)
+        finish_mean(0, 256, 5)
+        gather(D - 1, 256, 512)
+        finish_mean(256, 384, 0)
+        finish_mean(384, 512, 1)
+
+        def flat(tile, v0, v1):
+            return tile[:, v0:v1].rearrange("p v t -> p (v t)")
+
+        running = {MAX: rounded[0], MIN: rounded[0]}
+        for d in (1, 2):
+            for name, op in (("max", MAX), ("min", MIN)):
+                step = keep.tile([P, T, PACK], BF16, name="%s%d" % (name, d))
+                nc.vector.tensor_tensor(flat(step, 0, T), flat(running[op], 0, T), flat(rounded[d], 0, T), op)
+                running[op] = step
+
+        out_banks = ((6, 7), (2, 5), (3, 0))
+        for c, (v0, v1) in enumerate(PIECES):
+            width = v1 - v0
+            stats = {0: flat(mean, v0, v1)}
             for s, op in ((1, MAX), (2, MIN)):
-                pair = keep.tile([P, 2 * width], BF16, name="pair%d_%d" % (c, s))
-                nc.vector.tensor_tensor(pair[:], low, high, op)
-                halves.append(pair)
-            for s, op in ((1, MAX), (2, MIN)):
-                zs = keep.tile([P, width], BF16, name="stat%d_%d" % (c, s), align_bytes=64)
-                nc.vector.tensor_tensor(zs[:], halves[s - 1][:, :width], halves[s - 1][:, width:], op)
-                stats.append(zs[:])
-            acc = [psum_b.tile([P, CHUNK], F32, name="bank_b", tag="bank_b") for m in range(2)]
+                zs = keep.tile([P, width * PACK], BF16, name="stat%d_%d" % (c, s), align_bytes=64)
+                nc.vector.tensor_tensor(zs[:], flat(running[op], v0, v1), flat(rounded[D - 1], v0, v1), op)
+                stats[s] = zs[:]
+            acc = [bank(out_banks[c][m], [P, width]) for m in range(2)]
             for s in range(3):
-                codes = keep.tile([P, CHUNK], U32, name="z_codes%d_%d" % (c, s), align_bytes=64)
-                plane = keep.tile([P, CHUNK], U8, name="z_plane%d_%d" % (c, s), align_bytes=64)
+                codes = keep.tile([P, width], U32, name="z_codes%d_%d" % (c, s), align_bytes=64)
+                plane = keep.tile([P, width], U8, name="z_plane%d_%d" % (c, s), align_bytes=64)
                 nc.vector.quantize_mx(out=codes[:].bitcast(FP8X4), scales=plane[:], in_=stats[s])
                 for m in range(2):
                     nc.tensor.matmul_mx(
@@ -194,9 +219,14 @@ def tile_picked_wpna_none_l_kernel(
                         stop=(s == 2),
                     )
             for m in range(2):
-                result = keep.tile([P, CHUNK], F32, name="result%d_%d" % (c, m))
-                if c == CHUNKS - 1 and m == 1:
+                result = keep.tile([P, width], F32, name="result%d_%d" % (c, m))
+                rows = out[m * P : (m + 1) * P, v0:v1]
+                if c == len(PIECES) - 1 and m == 1:
                     nc.vector.tensor_copy(result[:], acc[m][:])
+                    nc.sync.dma_start(rows, result[:])
+                elif c == len(PIECES) - 1:
+                    nc.scalar.copy(result[:], acc[m][:])
+                    nc.scalar.dma_start(rows, result[:])
                 else:
                     nc.scalar.copy(result[:], acc[m][:])
-                nc.sync.dma_start(out[m * P : (m + 1) * P, c * CHUNK : (c + 1) * CHUNK], result[:])
+                    nc.sync.dma_start(rows, result[:])

@@ -36,18 +36,17 @@ def tile_picked_wpna_none_l_kernel(
             return psum.tile(shape, F32, name="bank%d" % b, tag="bank%d" % b)
 
         lists = [keep.tile([P, T // 16], U16, name="list%d" % d) for d in range(D)]
-        x_codes = keep.tile([P, 2, T], U32, name="x_codes", align_bytes=64)
-        x_plane = keep.tile([P, 2, T], U8, name="x_plane", align_bytes=64)
+        x_codes = [keep.tile([P, T], U32, name="x_codes%d" % z, align_bytes=64) for z in range(2)]
+        packed = keep.tile([P, T], U8, name="packed", align_bytes=64)
         h = keep.tile([P, (PACK - 1) * T + WINDOW], F32, name="h")
-        nc.gpsimd.memset(x_plane[:].bitcast(I32), 0)
         nc.gpsimd.memset(h[:, PACK * T :], 0.0)
 
         def plane_start(t):
             return (PACK - 1 - t) * T
 
-        def load_x(c0, c1):
-            words = x_words.rearrange("z p n t -> p z (n t)")[:, :, PACK * c0 : PACK * c1]
-            nc.sync.dma_start(x_codes[:, :, c0:c1].bitcast(I32), words.bitcast(I32))
+        def load_x(z):
+            words = x_words[z].rearrange("p n t -> p (n t)")
+            nc.sync.dma_start(x_codes[z][:].bitcast(I32), words.bitcast(I32))
 
         def load_w1(z, c0, c1):
             raw = keep.tile([P, PACK, c1 - c0], F32, name="w1_raw%d_%d" % (z, c0))
@@ -57,13 +56,11 @@ def tile_picked_wpna_none_l_kernel(
 
         w1_raw = {}
         w1_raw[0, 0] = load_w1(0, 0, 512)
-        w1_raw[1, 0] = load_w1(1, 0, 256)
-        scale_rows = x_scales.rearrange("z (q r) n -> q r z n", r=4)
         for q in range(4):
-            nc.sync.dma_start(x_plane[32 * q : 32 * q + 4, :, :].bitcast(I32), scale_rows[q].bitcast(I32))
-        w1_raw[1, 256] = load_w1(1, 256, 512)
-        load_x(0, 256)
-        load_x(256, 512)
+            nc.sync.dma_start(packed[32 * q : 32 * q + 8, :].bitcast(I32), x_scales[:, 4 * q : 4 * q + 4, :].bitcast(I32))
+        w1_raw[1, 0] = load_w1(1, 0, 512)
+        load_x(0)
+        load_x(1)
         for d, pos in enumerate((pos1, pos2, pos3, pos4)):
             nc.sync.dma_start(lists[d][:], pos)
         w_raw = []
@@ -77,63 +74,66 @@ def tile_picked_wpna_none_l_kernel(
 
         w1_bf = [keep.tile([P, PACK, P, PACK], BF16, name="w1_bf%d" % z, align_bytes=64) for z in range(2)]
         w1_codes = [keep.tile([P, PACK, P], U32, name="w1_codes%d" % z, align_bytes=64) for z in range(2)]
-        w1_plane = [keep.tile([P, PACK, P], U8, name="w1_plane%d" % z, align_bytes=64) for z in range(2)]
+        w1_plane1 = keep.tile([P, T], U8, name="w1_plane1", align_bytes=64)
+        w1_plane = [packed[8:P, :], w1_plane1[:]]
 
-        def cast_w1(z, c0, c1):
-            raw = w1_raw[z, c0]
-            ms = (c1 - c0) // PACK
-            split = ms * 3 // 4
-            src = raw[:].rearrange("p j (m t) -> p m j t", t=PACK)
-            dst = w1_bf[z][:, :, c0 // PACK : c1 // PACK, :].rearrange("p t m j -> p m j t")
-            nc.vector.tensor_copy(dst[:, :split], src[:, :split])
-            nc.scalar.activation(dst[:, split:], src[:, split:], COPY)
+        def cast_w1(z):
+            src = w1_raw[z, 0][:].rearrange("p j (m t) -> p m j t", t=PACK)
+            dst = w1_bf[z][:].rearrange("p t m j -> p m j t")
+            nc.vector.tensor_copy(dst[:, :, :, 0:2], src[:, :, :, 0:2])
+            nc.scalar.activation(dst[:, :, :, 2:4], src[:, :, :, 2:4], COPY)
 
         def quantize_w1(z, t0, t1):
             nc.vector.quantize_mx(
                 out=w1_codes[z][:, t0:t1, :].rearrange("p t m -> p (t m)").bitcast(FP8X4),
-                scales=w1_plane[z][:, t0:t1, :].rearrange("p t m -> p (t m)"),
+                scales=w1_plane[z][:, t0 * P : t1 * P],
                 in_=w1_bf[z][:, t0:t1].rearrange("p t m j -> p (t m j)"),
             )
 
-        cast_w1(0, 0, 512)
+        cast_w1(0)
         quantize_w1(0, 0, 4)
-        cast_w1(1, 0, 256)
-        cast_w1(1, 256, 512)
+        cast_w1(1)
         quantize_w1(1, 0, 1)
         quantize_w1(1, 1, 2)
         quantize_w1(1, 2, 4)
 
-        def first_product(b, t, c0, c1, engine_copy):
-            acc = bank(b, [P, c1 - c0])
-            for z in range(2):
-                nc.tensor.matmul_mx(
-                    acc[:],
-                    lhsT=w1_codes[z][:, t, :].bitcast(FP8X4),
-                    lhsT_scale=w1_plane[z][:, t, :],
-                    rhs=x_codes[:, z, c0:c1].bitcast(FP8X4),
-                    rhs_scale=x_plane[:, z, c0:c1],
-                    start=(z == 0),
-                    stop=(z == 1),
-                )
-            engine_copy(h[:, plane_start(t) + c0 : plane_start(t) + c1], acc[:])
+        def first_pass(acc, z, t, c0, c1, start):
+            nc.tensor.matmul_mx(
+                acc[:],
+                lhsT=w1_codes[z][:, t, :].bitcast(FP8X4),
+                lhsT_scale=w1_plane[z][:, t * P : (t + 1) * P],
+                rhs=x_codes[z][:, c0:c1].bitcast(FP8X4),
+                rhs_scale=packed[4 * z : P, c0:c1],
+                start=start,
+                stop=not start,
+            )
 
-        first_product(0, 0, 0, 256, nc.scalar.copy)
-        first_product(1, 0, 256, 512, nc.vector.tensor_copy)
+        halves = [bank(b, [P, T // 2]) for b in range(2)]
+        for z in range(2):
+            for b in range(2):
+                first_pass(halves[b], z, 0, b * T // 2, (b + 1) * T // 2, z == 0)
+        nc.scalar.copy(h[:, plane_start(0) : plane_start(0) + T // 2], halves[0][:])
+        nc.vector.tensor_copy(h[:, plane_start(0) + T // 2 : plane_start(0) + T], halves[1][:])
         for t in range(1, PACK):
-            first_product(1 + t, t, 0, T, nc.scalar.copy)
+            acc = bank(1 + t, [P, T])
+            first_pass(acc, 1, t, 0, T, True)
+            first_pass(acc, 0, t, 0, T, False)
+            nc.scalar.copy(h[:, plane_start(t) : plane_start(t) + T], acc[:])
 
-        w_codes, w_plane = [], []
+        w_bf = keep.tile([P, 3, N, PACK], BF16, name="w_bf", align_bytes=64)
+        w_codes = keep.tile([P, 3 * N], U32, name="w_codes", align_bytes=64)
+        w_plane = keep.tile([P, 3 * N], U8, name="w_plane", align_bytes=64)
         for s in range(3):
-            bf = keep.tile([P, N, PACK], BF16, name="w_bf%d" % s, align_bytes=64)
             nc.scalar.copy(
-                bf[:].rearrange("p (c i) j -> p c j i", i=4),
+                w_bf[:, s].rearrange("p (c i) j -> p c j i", i=4),
                 w_raw[s][:].rearrange("p j (c i) -> p c j i", i=4),
             )
-            codes = keep.tile([P, N], U32, name="w_codes%d" % s, align_bytes=64)
-            plane = keep.tile([P, N], U8, name="w_plane%d" % s, align_bytes=64)
-            nc.vector.quantize_mx(out=codes[:].bitcast(FP8X4), scales=plane[:], in_=bf[:].rearrange("p n j -> p (n j)"))
-            w_codes.append(codes)
-            w_plane.append(plane)
+        for s0, s1 in ((0, 2), (2, 3)):
+            nc.vector.quantize_mx(
+                out=w_codes[:, s0 * N : s1 * N].bitcast(FP8X4),
+                scales=w_plane[:, s0 * N : s1 * N],
+                in_=w_bf[:, s0:s1].rearrange("p s n j -> p (s n j)"),
+            )
 
         totals = [bank(1 + b, [P, PACK, P]) for b in range(T // P)]
         rounded = [keep.tile([P, T, PACK], BF16, name="rounded%d" % d, align_bytes=64) for d in range(D)]
@@ -153,9 +153,12 @@ def tile_picked_wpna_none_l_kernel(
                         start=(d == 0 and t == 0),
                         stop=(d == D - 1 and t == PACK - 1),
                     )
+            return g
+
+        def round_picked(d, g, v0, v1):
             nc.scalar.copy(
                 rounded[d][:, v0:v1].rearrange("p (c i) t -> p c t i", i=4),
-                g[:].rearrange("p t (c i) -> p c t i", i=4),
+                g[:, :, v0:v1].rearrange("p t (c i) -> p c t i", i=4),
             )
 
         mean = keep.tile([P, T, PACK], BF16, name="mean", align_bytes=64)
@@ -178,10 +181,11 @@ def tile_picked_wpna_none_l_kernel(
             )
 
         for d in range(D - 1):
-            gather(d, 0, T)
-        gather(D - 1, 0, 256)
+            round_picked(d, gather(d, 0, T), 0, T)
+        last = gather(D - 1, 0, T)
+        round_picked(D - 1, last, 0, 256)
         finish_mean(0, 256, 5)
-        gather(D - 1, 256, 512)
+        round_picked(D - 1, last, 256, 512)
         finish_mean(256, 384, 0)
         finish_mean(384, 512, 1)
 
@@ -198,33 +202,46 @@ def tile_picked_wpna_none_l_kernel(
         out_banks = ((6, 7), (2, 5), (3, 0))
         for c, (v0, v1) in enumerate(PIECES):
             width = v1 - v0
-            stats = {0: flat(mean, v0, v1)}
-            for s, op in ((1, MAX), (2, MIN)):
-                zs = keep.tile([P, width * PACK], BF16, name="stat%d_%d" % (c, s), align_bytes=64)
-                nc.vector.tensor_tensor(zs[:], flat(running[op], v0, v1), flat(rounded[D - 1], v0, v1), op)
-                stats[s] = zs[:]
+            final = c == len(PIECES) - 1
+            extremes = keep.tile([P, 2, width * PACK], BF16, name="extremes%d" % c, align_bytes=64)
+            for s, op in enumerate((MAX, MIN)):
+                nc.vector.tensor_tensor(extremes[:, s], flat(running[op], v0, v1), flat(rounded[D - 1], v0, v1), op)
+            codes = keep.tile([P, 3 * width], U32, name="z_codes%d" % c, align_bytes=64)
+            plane = keep.tile([P, 3 * width], U8, name="z_plane%d" % c, align_bytes=64)
+
+            def quantize_z(s0, s1, values):
+                nc.vector.quantize_mx(
+                    out=codes[:, s0 * width : s1 * width].bitcast(FP8X4),
+                    scales=plane[:, s0 * width : s1 * width],
+                    in_=values,
+                )
+
+            quantize_z(0, 1, flat(mean, v0, v1))
+            if final:
+                quantize_z(1, 2, extremes[:, 0])
+                quantize_z(2, 3, extremes[:, 1])
+            else:
+                quantize_z(1, 3, extremes[:].rearrange("p s w -> p (s w)"))
             acc = [bank(out_banks[c][m], [P, width]) for m in range(2)]
             for s in range(3):
-                codes = keep.tile([P, width], U32, name="z_codes%d_%d" % (c, s), align_bytes=64)
-                plane = keep.tile([P, width], U8, name="z_plane%d_%d" % (c, s), align_bytes=64)
-                nc.vector.quantize_mx(out=codes[:].bitcast(FP8X4), scales=plane[:], in_=stats[s])
                 for m in range(2):
+                    cols = slice(s * N + m * P, s * N + (m + 1) * P)
                     nc.tensor.matmul_mx(
                         acc[m][:],
-                        lhsT=w_codes[s][:, m * P : (m + 1) * P].bitcast(FP8X4),
-                        lhsT_scale=w_plane[s][:, m * P : (m + 1) * P],
-                        rhs=codes[:].bitcast(FP8X4),
-                        rhs_scale=plane[:],
+                        lhsT=w_codes[:, cols].bitcast(FP8X4),
+                        lhsT_scale=w_plane[:, cols],
+                        rhs=codes[:, s * width : (s + 1) * width].bitcast(FP8X4),
+                        rhs_scale=plane[:, s * width : (s + 1) * width],
                         start=(s == 0),
                         stop=(s == 2),
                     )
             for m in range(2):
                 result = keep.tile([P, width], F32, name="result%d_%d" % (c, m))
                 rows = out[m * P : (m + 1) * P, v0:v1]
-                if c == len(PIECES) - 1 and m == 1:
+                if final and m == 1:
                     nc.vector.tensor_copy(result[:], acc[m][:])
                     nc.sync.dma_start(rows, result[:])
-                elif c == len(PIECES) - 1:
+                elif final:
                     nc.scalar.copy(result[:], acc[m][:])
                     nc.scalar.dma_start(rows, result[:])
                 else:

@@ -16,11 +16,15 @@ FP8X4 = mybir.dt.float8_e4m3fn_x4
 COPY = mybir.ActivationFunctionType.Copy
 MAX = mybir.AluOpType.max
 MIN = mybir.AluOpType.min
+ADD = mybir.AluOpType.add
+SUBTRACT = mybir.AluOpType.subtract
+RELU = mybir.ActivationFunctionType.Relu
 
 P = 128
 PACK = 4
 D = 4
 WINDOW = 704
+SHARE = 256
 PIECES = ((0, 256), (256, 384), (384, 512))
 
 
@@ -38,11 +42,13 @@ def tile_picked_wpna_none_l_kernel(
         lists = [keep.tile([P, T // 16], U16, name="list%d" % d) for d in range(D)]
         x_codes = [keep.tile([P, T], U32, name="x_codes%d" % z, align_bytes=64) for z in range(2)]
         packed = keep.tile([P, T], U8, name="packed", align_bytes=64)
-        h = keep.tile([P, (PACK - 1) * T + WINDOW], F32, name="h")
-        nc.gpsimd.memset(h[:, PACK * T :], 0.0)
+        h = keep.tile([P, 2 * T + 2 * WINDOW], F32, name="h")
 
         def plane_start(t):
-            return (PACK - 1 - t) * T
+            return (2 - t) * T if t < 3 else 2 * T + WINDOW
+
+        for t in (0, 3):
+            nc.gpsimd.memset(h[:, plane_start(t) + T : plane_start(t) + WINDOW], 0.0)
 
         def load_x(z):
             words = x_words[z].rearrange("p n t -> p (n t)")
@@ -73,7 +79,7 @@ def tile_picked_wpna_none_l_kernel(
         make_identity(nc, identity[:])
 
         w1_bf = [keep.tile([P, PACK, P, PACK], BF16, name="w1_bf%d" % z, align_bytes=64) for z in range(2)]
-        w1_codes = [keep.tile([P, PACK, P], U32, name="w1_codes%d" % z, align_bytes=64) for z in range(2)]
+        w1_codes = [keep.tile([P, PACK, P], U32, name="w1_codes%d" % z, tag="reuse%d" % z, align_bytes=64) for z in range(2)]
         w1_plane1 = keep.tile([P, T], U8, name="w1_plane1", align_bytes=64)
         w1_plane = [packed[8:P, :], w1_plane1[:]]
 
@@ -120,29 +126,15 @@ def tile_picked_wpna_none_l_kernel(
             first_pass(acc, 0, t, 0, T, False)
             nc.scalar.copy(h[:, plane_start(t) : plane_start(t) + T], acc[:])
 
-        w_bf = keep.tile([P, 3, N, PACK], BF16, name="w_bf", align_bytes=64)
-        w_codes = keep.tile([P, 3 * N], U32, name="w_codes", align_bytes=64)
-        w_plane = keep.tile([P, 3 * N], U8, name="w_plane", align_bytes=64)
-        for s in range(3):
-            nc.scalar.copy(
-                w_bf[:, s].rearrange("p (c i) j -> p c j i", i=4),
-                w_raw[s][:].rearrange("p j (c i) -> p c j i", i=4),
-            )
-        for s0, s1 in ((0, 2), (2, 3)):
-            nc.vector.quantize_mx(
-                out=w_codes[:, s0 * N : s1 * N].bitcast(FP8X4),
-                scales=w_plane[:, s0 * N : s1 * N],
-                in_=w_bf[:, s0:s1].rearrange("p s n j -> p (s n j)"),
-            )
-
         totals = [bank(1 + b, [P, PACK, P]) for b in range(T // P)]
-        rounded = [keep.tile([P, T, PACK], BF16, name="rounded%d" % d, align_bytes=64) for d in range(D)]
+        rounded = {}
 
         def gather(d, v0, v1):
             g = keep.tile([P, PACK, v1 - v0], F32, name="picked%d_%d" % (d, v0))
             offsets = lists[d][:, v0 // 16 : v1 // 16]
             for t in range(PACK):
-                window = h[:, plane_start(t) : plane_start(t) + WINDOW]
+                end = plane_start(t) + WINDOW if d == 0 or (d == 1 and v0 == 0) or t == 3 else plane_start(3) + 8
+                window = h[:, plane_start(t) : end]
                 nc.vector.tensor_copy(g[:, t, :], window.indirect(offsets))
                 for b in range(v0 // P, v1 // P):
                     nc.tensor.matmul(
@@ -155,11 +147,14 @@ def tile_picked_wpna_none_l_kernel(
                     )
             return g
 
-        def round_picked(d, g, v0, v1):
+        def round_picked(d, g, v0, v1, first=0):
             nc.scalar.copy(
                 rounded[d][:, v0:v1].rearrange("p (c i) t -> p c t i", i=4),
-                g[:, :, v0:v1].rearrange("p t (c i) -> p c t i", i=4),
+                g[:, :, v0 - first : v1 - first].rearrange("p t (c i) -> p c t i", i=4),
             )
+
+        def flat(tile, v0, v1):
+            return tile[:, v0:v1].rearrange("p v t -> p (v t)")
 
         mean = keep.tile([P, T, PACK], BF16, name="mean", align_bytes=64)
 
@@ -180,8 +175,42 @@ def tile_picked_wpna_none_l_kernel(
                 back[:].rearrange("p b u v -> p b v u"),
             )
 
-        for d in range(D - 1):
-            round_picked(d, gather(d, 0, T), 0, T)
+        for d in (0, 1, 3):
+            rounded[d] = keep.tile([P, T, PACK], BF16, name="rounded%d" % d, align_bytes=64)
+        first = gather(0, 0, T)
+        round_picked(0, first, 0, 256)
+        round_picked(1, gather(1, 0, 256), 0, 256)
+        max01 = keep.tile([P, T, PACK], BF16, name="max01")
+        min01 = keep.tile([P, T, PACK], BF16, name="min01")
+        gap = keep.tile([P, SHARE, PACK], F32, name="gap", tag="late", align_bytes=64)
+        excess = keep.tile([P, SHARE, PACK], F32, name="excess")
+        parts = ((0, SHARE // 2), (SHARE // 2, SHARE))
+        for v0, v1 in parts:
+            nc.gpsimd.tensor_tensor(flat(gap, v0, v1), flat(rounded[1], v0, v1), flat(rounded[0], v0, v1), SUBTRACT)
+        for v0, v1 in parts:
+            nc.scalar.activation(flat(excess, v0, v1), flat(gap, v0, v1), RELU)
+        round_picked(0, first, 256, T)
+        round_picked(1, gather(1, 256, T), 256, T, 256)
+        for v0, v1 in parts:
+            nc.gpsimd.tensor_tensor(flat(max01, v0, v1), flat(rounded[0], v0, v1), flat(excess, v0, v1), ADD)
+            nc.gpsimd.tensor_tensor(flat(min01, v0, v1), flat(rounded[1], v0, v1), flat(excess, v0, v1), SUBTRACT)
+        w_bf = keep.tile([P, 3, N, PACK], BF16, name="w_bf", tag="reuse0", align_bytes=64)
+        w_codes = keep.tile([P, 3 * N], U32, name="w_codes", align_bytes=64)
+        w_plane = keep.tile([P, 3 * N], U8, name="w_plane", align_bytes=64)
+        for s in range(3):
+            nc.scalar.copy(
+                w_bf[:, s].rearrange("p (c i) j -> p c j i", i=4),
+                w_raw[s][:].rearrange("p j (c i) -> p c j i", i=4),
+            )
+        for s0, s1 in ((0, 2), (2, 3)):
+            nc.vector.quantize_mx(
+                out=w_codes[:, s0 * N : s1 * N].bitcast(FP8X4),
+                scales=w_plane[:, s0 * N : s1 * N],
+                in_=w_bf[:, s0:s1].rearrange("p s n j -> p (s n j)"),
+            )
+
+        rounded[2] = keep.tile([P, T, PACK], BF16, name="rounded2", tag="late", align_bytes=64)
+        round_picked(2, gather(2, 0, T), 0, T)
         last = gather(D - 1, 0, T)
         round_picked(D - 1, last, 0, 256)
         finish_mean(0, 256, 5)
@@ -189,15 +218,13 @@ def tile_picked_wpna_none_l_kernel(
         finish_mean(256, 384, 0)
         finish_mean(384, 512, 1)
 
-        def flat(tile, v0, v1):
-            return tile[:, v0:v1].rearrange("p v t -> p (v t)")
-
-        running = {MAX: rounded[0], MIN: rounded[0]}
-        for d in (1, 2):
-            for name, op in (("max", MAX), ("min", MIN)):
-                step = keep.tile([P, T, PACK], BF16, name="%s%d" % (name, d))
-                nc.vector.tensor_tensor(flat(step, 0, T), flat(running[op], 0, T), flat(rounded[d], 0, T), op)
-                running[op] = step
+        running = {}
+        for op, both in ((MAX, max01), (MIN, min01)):
+            nc.vector.tensor_tensor(flat(both, SHARE, T), flat(rounded[0], SHARE, T), flat(rounded[1], SHARE, T), op)
+        for name, op, both in (("max", MAX, max01), ("min", MIN, min01)):
+            step = keep.tile([P, T, PACK], BF16, name="%s012" % name)
+            nc.vector.tensor_tensor(flat(step, 0, T), flat(both, 0, T), flat(rounded[2], 0, T), op)
+            running[op] = step
 
         out_banks = ((6, 7), (2, 5), (3, 0))
         for c, (v0, v1) in enumerate(PIECES):

@@ -24,7 +24,8 @@ P = 128
 PACK = 4
 D = 4
 WINDOW = 704
-SHARE = 256
+WHOLE = 1024
+HALF = 256
 PIECES = ((0, 256), (256, 384), (384, 512))
 
 
@@ -42,13 +43,9 @@ def tile_picked_wpna_none_l_kernel(
         lists = [keep.tile([P, T // 16], U16, name="list%d" % d) for d in range(D)]
         x_codes = [keep.tile([P, T], U32, name="x_codes%d" % z, align_bytes=64) for z in range(2)]
         packed = keep.tile([P, T], U8, name="packed", align_bytes=64)
-        h = keep.tile([P, 2 * T + 2 * WINDOW], F32, name="h")
-
-        def plane_start(t):
-            return (2 - t) * T if t < 3 else 2 * T + WINDOW
-
-        for t in (0, 3):
-            nc.gpsimd.memset(h[:, plane_start(t) + T : plane_start(t) + WINDOW], 0.0)
+        h = [keep.tile([P, WHOLE], F32, name="h%d" % t) for t in range(PACK)]
+        for t in range(PACK):
+            nc.gpsimd.memset(h[t][:, T:WHOLE], 0.0)
 
         def load_x(z):
             words = x_words[z].rearrange("p n t -> p (n t)")
@@ -118,33 +115,34 @@ def tile_picked_wpna_none_l_kernel(
         for z in range(2):
             for b in range(2):
                 first_pass(halves[b], z, 0, b * T // 2, (b + 1) * T // 2, z == 0)
-        nc.scalar.copy(h[:, plane_start(0) : plane_start(0) + T // 2], halves[0][:])
-        nc.vector.tensor_copy(h[:, plane_start(0) + T // 2 : plane_start(0) + T], halves[1][:])
+        nc.scalar.copy(h[0][:, 0 : T // 2], halves[0][:])
+        nc.vector.tensor_copy(h[0][:, T // 2 : T], halves[1][:])
         for t in range(1, PACK):
             acc = bank(1 + t, [P, T])
             first_pass(acc, 1, t, 0, T, True)
             first_pass(acc, 0, t, 0, T, False)
-            nc.scalar.copy(h[:, plane_start(t) : plane_start(t) + T], acc[:])
+            nc.scalar.copy(h[t][:, 0:T], acc[:])
 
         totals = [bank(1 + b, [P, PACK, P]) for b in range(T // P)]
         rounded = {}
 
+        def add_turned(values, t, v0, v1, start=False, stop=False):
+            for b in range(v0 // P, v1 // P):
+                nc.tensor.matmul(
+                    totals[b][:, t, :],
+                    lhsT=values[:, b * P - v0 : (b + 1) * P - v0],
+                    rhs=identity[:],
+                    is_transpose=True,
+                    start=start,
+                    stop=stop,
+                )
+
         def gather(d, v0, v1):
-            g = keep.tile([P, PACK, v1 - v0], F32, name="picked%d_%d" % (d, v0))
+            g = picked[:, d - 2, :, v0:v1]
             offsets = lists[d][:, v0 // 16 : v1 // 16]
             for t in range(PACK):
-                end = plane_start(t) + WINDOW if d == 0 or (d == 1 and v0 == 0) or t == 3 else plane_start(3) + 8
-                window = h[:, plane_start(t) : end]
-                nc.vector.tensor_copy(g[:, t, :], window.indirect(offsets))
-                for b in range(v0 // P, v1 // P):
-                    nc.tensor.matmul(
-                        totals[b][:, t, :],
-                        lhsT=g[:, t, b * P - v0 : (b + 1) * P - v0],
-                        rhs=identity[:],
-                        is_transpose=True,
-                        start=(d == 0 and t == 0),
-                        stop=(d == D - 1 and t == PACK - 1),
-                    )
+                nc.vector.tensor_copy(g[:, t, :], h[t][:, 0:WINDOW].indirect(offsets))
+                add_turned(g[:, t, :], t, v0, v1, stop=(d == D - 1 and t == PACK - 1))
             return g
 
         def round_picked(d, g, v0, v1, first=0):
@@ -175,25 +173,6 @@ def tile_picked_wpna_none_l_kernel(
                 back[:].rearrange("p b u v -> p b v u"),
             )
 
-        for d in (0, 1, 3):
-            rounded[d] = keep.tile([P, T, PACK], BF16, name="rounded%d" % d, align_bytes=64)
-        first = gather(0, 0, T)
-        round_picked(0, first, 0, 256)
-        round_picked(1, gather(1, 0, 256), 0, 256)
-        max01 = keep.tile([P, T, PACK], BF16, name="max01")
-        min01 = keep.tile([P, T, PACK], BF16, name="min01")
-        gap = keep.tile([P, SHARE, PACK], F32, name="gap", tag="late", align_bytes=64)
-        excess = keep.tile([P, SHARE, PACK], F32, name="excess")
-        parts = ((0, SHARE // 2), (SHARE // 2, SHARE))
-        for v0, v1 in parts:
-            nc.gpsimd.tensor_tensor(flat(gap, v0, v1), flat(rounded[1], v0, v1), flat(rounded[0], v0, v1), SUBTRACT)
-        for v0, v1 in parts:
-            nc.scalar.activation(flat(excess, v0, v1), flat(gap, v0, v1), RELU)
-        round_picked(0, first, 256, T)
-        round_picked(1, gather(1, 256, T), 256, T, 256)
-        for v0, v1 in parts:
-            nc.gpsimd.tensor_tensor(flat(max01, v0, v1), flat(rounded[0], v0, v1), flat(excess, v0, v1), ADD)
-            nc.gpsimd.tensor_tensor(flat(min01, v0, v1), flat(rounded[1], v0, v1), flat(excess, v0, v1), SUBTRACT)
         w_bf = keep.tile([P, 3, N, PACK], BF16, name="w_bf", tag="reuse0", align_bytes=64)
         w_codes = keep.tile([P, 3 * N], U32, name="w_codes", align_bytes=64)
         w_plane = keep.tile([P, 3 * N], U8, name="w_plane", align_bytes=64)
@@ -202,34 +181,65 @@ def tile_picked_wpna_none_l_kernel(
                 w_bf[:, s].rearrange("p (c i) j -> p c j i", i=4),
                 w_raw[s][:].rearrange("p j (c i) -> p c j i", i=4),
             )
+
+        first = keep.tile([P, PACK, T], F32, name="first")
+        gap = keep.tile([P, PACK, T], F32, name="gap")
+        above = keep.tile([P, PACK, T], F32, name="above")
+        below = keep.tile([P, PACK, T], F32, name="below")
+        for t in range(PACK):
+            nc.vector.tensor_copy(first[:, t, :], h[t][:, 0:WINDOW].indirect(lists[0][:]))
+            nc.vector.tensor_tensor(gap[:, t, :], h[t][:].indirect(lists[1][:]), first[:, t, :], SUBTRACT)
+            add_turned(first[:, t, :], t, 0, T, start=(t == 0))
+            add_turned(first[:, t, :], t, 0, T)
+            add_turned(gap[:, t, :], t, 0, T)
+            nc.scalar.activation(above[:, t, :], gap[:, t, :], RELU)
+            nc.scalar.activation(below[:, t, :], gap[:, t, :], RELU, scale=-1.0)
         for s0, s1 in ((0, 2), (2, 3)):
             nc.vector.quantize_mx(
                 out=w_codes[:, s0 * N : s1 * N].bitcast(FP8X4),
                 scales=w_plane[:, s0 * N : s1 * N],
                 in_=w_bf[:, s0:s1].rearrange("p s n j -> p (s n j)"),
             )
+        max01 = keep.tile([P, 2, T, 2], BF16, name="max01")
+        min01 = keep.tile([P, 2, T, 2], BF16, name="min01")
+        for v0 in range(0, T, HALF):
+            for both, part, op in ((max01, above, ADD), (min01, below, SUBTRACT)):
+                nc.gpsimd.tensor_tensor(
+                    both[:, :, v0 : v0 + HALF].rearrange("p u v e -> p u e v"),
+                    first[:, :, v0 : v0 + HALF].rearrange("p (u e) v -> p u e v", e=2),
+                    part[:, :, v0 : v0 + HALF].rearrange("p (u e) v -> p u e v", e=2),
+                    op,
+                )
 
-        rounded[2] = keep.tile([P, T, PACK], BF16, name="rounded2", tag="late", align_bytes=64)
+        picked = keep.tile([P, 2, PACK, T], F32, name="picked", tag="reuse0", align_bytes=64)
+        for d in (2, 3):
+            rounded[d] = keep.tile([P, T, PACK], BF16, name="rounded%d" % d, align_bytes=64)
         round_picked(2, gather(2, 0, T), 0, T)
-        last = gather(D - 1, 0, T)
-        round_picked(D - 1, last, 0, 256)
+        round_picked(3, gather(3, 0, 256), 0, 256)
         finish_mean(0, 256, 5)
-        round_picked(D - 1, last, 256, 512)
+        round_picked(3, gather(3, 256, T), 256, T, 256)
         finish_mean(256, 384, 0)
         finish_mean(384, 512, 1)
 
         running = {}
-        for op, both in ((MAX, max01), (MIN, min01)):
-            nc.vector.tensor_tensor(flat(both, SHARE, T), flat(rounded[0], SHARE, T), flat(rounded[1], SHARE, T), op)
-        for name, op, both in (("max", MAX, max01), ("min", MIN, min01)):
-            step = keep.tile([P, T, PACK], BF16, name="%s012" % name)
-            nc.vector.tensor_tensor(flat(step, 0, T), flat(both, 0, T), flat(rounded[2], 0, T), op)
-            running[op] = step
+        for name, op in (("max", MAX), ("min", MIN)):
+            running[op] = keep.tile([P, T, PACK], BF16, name="%s012" % name)
+
+        def second_level(v0, v1):
+            for op, both in ((MAX, max01), (MIN, min01)):
+                nc.vector.tensor_tensor(
+                    running[op][:, v0:v1].rearrange("p v (u e) -> p v u e", e=2),
+                    both[:, :, v0:v1].rearrange("p u v e -> p v u e"),
+                    rounded[2][:, v0:v1].rearrange("p v (u e) -> p v u e", e=2),
+                    op,
+                )
 
         out_banks = ((6, 7), (2, 5), (3, 0))
         for c, (v0, v1) in enumerate(PIECES):
             width = v1 - v0
             final = c == len(PIECES) - 1
+            if v0 % HALF == 0:
+                second_level(v0, v0 + HALF)
             extremes = keep.tile([P, 2, width * PACK], BF16, name="extremes%d" % c, align_bytes=64)
             for s, op in enumerate((MAX, MIN)):
                 nc.vector.tensor_tensor(extremes[:, s], flat(running[op], v0, v1), flat(rounded[D - 1], v0, v1), op)

@@ -118,12 +118,12 @@ def tile_picked_wpna_none_l_kernel(
         nc.scalar.copy(h[0][:, 0 : T // 2], halves[0][:])
         nc.vector.tensor_copy(h[0][:, T // 2 : T], halves[1][:])
         for t in range(1, PACK):
-            acc = bank(1 + t, [P, T])
+            acc = bank((1 + t) % 3, [P, T])
             first_pass(acc, 1, t, 0, T, True)
             first_pass(acc, 0, t, 0, T, False)
             nc.scalar.copy(h[t][:, 0:T], acc[:])
 
-        totals = [bank(1 + b, [P, PACK, P]) for b in range(T // P)]
+        totals = [bank(4 + b, [P, PACK, P]) for b in range(T // P)]
         rounded = {}
 
         def add_turned(values, t, v0, v1, start=False, stop=False):
@@ -137,8 +137,7 @@ def tile_picked_wpna_none_l_kernel(
                     stop=stop,
                 )
 
-        def gather(d, v0, v1):
-            g = picked[:, d - 2, :, v0:v1]
+        def gather(d, g, v0, v1):
             offsets = lists[d][:, v0 // 16 : v1 // 16]
             for t in range(PACK):
                 nc.vector.tensor_copy(g[:, t, :], h[t][:, 0:WINDOW].indirect(offsets))
@@ -173,6 +172,37 @@ def tile_picked_wpna_none_l_kernel(
                 back[:].rearrange("p b u v -> p b v u"),
             )
 
+        first = keep.tile([P, PACK, T], F32, name="first")
+        above = keep.tile([P, PACK, T], F32, name="above")
+        below = keep.tile([P, PACK, T], F32, name="below")
+        max01 = keep.tile([P, 2, T, 2], BF16, name="max01")
+        min01 = keep.tile([P, 2, T, 2], BF16, name="min01")
+
+        def gather_first(t):
+            nc.vector.tensor_copy(first[:, t, :], h[t][:, 0:WINDOW].indirect(lists[0][:]))
+            add_turned(first[:, t, :], t, 0, T, start=(t == 0))
+            add_turned(first[:, t, :], t, 0, T)
+
+        def gather_gap(t, gap):
+            nc.vector.tensor_tensor(gap, h[t][:].indirect(lists[1][:]), first[:, t, :], SUBTRACT)
+            add_turned(gap, t, 0, T)
+            nc.scalar.activation(above[:, t, :], gap, RELU)
+            nc.scalar.activation(below[:, t, :], gap, RELU, scale=-1.0)
+
+        def first_level(u):
+            for both, part, op in ((max01, above, ADD), (min01, below, SUBTRACT)):
+                nc.gpsimd.tensor_tensor(
+                    both[:, u].rearrange("p v e -> p e v"), first[:, 2 * u : 2 * u + 2], part[:, 2 * u : 2 * u + 2], op
+                )
+
+        early = keep.tile([P, 2, T], F32, name="early", tag="held")
+        for t in range(2):
+            gather_first(t)
+            gather_gap(t, early[:, t, :])
+        first_level(0)
+        for t in range(2, PACK):
+            gather_first(t)
+
         w_bf = keep.tile([P, 3, N, PACK], BF16, name="w_bf", tag="reuse0", align_bytes=64)
         w_codes = keep.tile([P, 3 * N], U32, name="w_codes", align_bytes=64)
         w_plane = keep.tile([P, 3 * N], U8, name="w_plane", align_bytes=64)
@@ -182,59 +212,41 @@ def tile_picked_wpna_none_l_kernel(
                 w_raw[s][:].rearrange("p j (c i) -> p c j i", i=4),
             )
 
-        first = keep.tile([P, PACK, T], F32, name="first")
-        gap = keep.tile([P, PACK, T], F32, name="gap")
-        above = keep.tile([P, PACK, T], F32, name="above")
-        below = keep.tile([P, PACK, T], F32, name="below")
-        for t in range(PACK):
-            nc.vector.tensor_copy(first[:, t, :], h[t][:, 0:WINDOW].indirect(lists[0][:]))
-            nc.vector.tensor_tensor(gap[:, t, :], h[t][:].indirect(lists[1][:]), first[:, t, :], SUBTRACT)
-            add_turned(first[:, t, :], t, 0, T, start=(t == 0))
-            add_turned(first[:, t, :], t, 0, T)
-            add_turned(gap[:, t, :], t, 0, T)
-            nc.scalar.activation(above[:, t, :], gap[:, t, :], RELU)
-            nc.scalar.activation(below[:, t, :], gap[:, t, :], RELU, scale=-1.0)
-        for s0, s1 in ((0, 2), (2, 3)):
+        for d in (3,):
+            rounded[d] = keep.tile([P, T, PACK], BF16, name="rounded%d" % d, align_bytes=64)
+        middle = keep.tile([P, PACK + 2, T], F32, name="middle", tag="held")
+        third = gather(2, middle[:, 0:PACK, :], 0, T)
+        paired = keep.tile([P, 2, T, 2], BF16, name="paired")
+        for u in range(2):
+            nc.scalar.copy(
+                paired[:, u].rearrange("p (c i) e -> p c e i", i=4),
+                third[:, 2 * u : 2 * u + 2].rearrange("p e (c i) -> p c e i", i=4),
+            )
+        for t in range(2, PACK):
+            gather_gap(t, middle[:, PACK + t - 2, :])
+        first_level(1)
+        for s0, s1 in ((2, 3), (0, 2)):
             nc.vector.quantize_mx(
                 out=w_codes[:, s0 * N : s1 * N].bitcast(FP8X4),
                 scales=w_plane[:, s0 * N : s1 * N],
                 in_=w_bf[:, s0:s1].rearrange("p s n j -> p (s n j)"),
             )
-        max01 = keep.tile([P, 2, T, 2], BF16, name="max01")
-        min01 = keep.tile([P, 2, T, 2], BF16, name="min01")
-        for v0 in range(0, T, HALF):
-            for both, part, op in ((max01, above, ADD), (min01, below, SUBTRACT)):
-                nc.gpsimd.tensor_tensor(
-                    both[:, :, v0 : v0 + HALF].rearrange("p u v e -> p u e v"),
-                    first[:, :, v0 : v0 + HALF].rearrange("p (u e) v -> p u e v", e=2),
-                    part[:, :, v0 : v0 + HALF].rearrange("p (u e) v -> p u e v", e=2),
-                    op,
-                )
-
-        picked = keep.tile([P, 2, PACK, T], F32, name="picked", tag="reuse0", align_bytes=64)
-        for d in (2, 3):
-            rounded[d] = keep.tile([P, T, PACK], BF16, name="rounded%d" % d, align_bytes=64)
-        round_picked(2, gather(2, 0, T), 0, T)
-        round_picked(3, gather(3, 0, 256), 0, 256)
-        finish_mean(0, 256, 5)
-        round_picked(3, gather(3, 256, T), 256, T, 256)
+        last = keep.tile([P, PACK, T], F32, name="last", tag="reuse0", align_bytes=64)
+        round_picked(3, gather(3, last[:, :, 0:HALF], 0, HALF), 0, HALF)
+        finish_mean(0, 256, 1)
+        round_picked(3, gather(3, last[:, :, HALF:T], HALF, T), HALF, T, HALF)
         finish_mean(256, 384, 0)
-        finish_mean(384, 512, 1)
+        finish_mean(384, 512, 4)
 
         running = {}
         for name, op in (("max", MAX), ("min", MIN)):
-            running[op] = keep.tile([P, T, PACK], BF16, name="%s012" % name)
+            running[op] = keep.tile([P, 2, T, 2], BF16, name="%s012" % name)
 
         def second_level(v0, v1):
             for op, both in ((MAX, max01), (MIN, min01)):
-                nc.vector.tensor_tensor(
-                    running[op][:, v0:v1].rearrange("p v (u e) -> p v u e", e=2),
-                    both[:, :, v0:v1].rearrange("p u v e -> p v u e"),
-                    rounded[2][:, v0:v1].rearrange("p v (u e) -> p v u e", e=2),
-                    op,
-                )
+                nc.vector.tensor_tensor(running[op][:, :, v0:v1], both[:, :, v0:v1], paired[:, :, v0:v1], op)
 
-        out_banks = ((6, 7), (2, 5), (3, 0))
+        out_banks = ((2, 3), (5, 1), (6, 0))
         for c, (v0, v1) in enumerate(PIECES):
             width = v1 - v0
             final = c == len(PIECES) - 1
@@ -242,7 +254,12 @@ def tile_picked_wpna_none_l_kernel(
                 second_level(v0, v0 + HALF)
             extremes = keep.tile([P, 2, width * PACK], BF16, name="extremes%d" % c, align_bytes=64)
             for s, op in enumerate((MAX, MIN)):
-                nc.vector.tensor_tensor(extremes[:, s], flat(running[op], v0, v1), flat(rounded[D - 1], v0, v1), op)
+                nc.vector.tensor_tensor(
+                    extremes[:, s].rearrange("p (v u e) -> p v u e", u=2, e=2),
+                    running[op][:, :, v0:v1].rearrange("p u v e -> p v u e"),
+                    rounded[D - 1][:, v0:v1].rearrange("p v (u e) -> p v u e", e=2),
+                    op,
+                )
             codes = keep.tile([P, 3 * width], U32, name="z_codes%d" % c, align_bytes=64)
             plane = keep.tile([P, 3 * width], U8, name="z_plane%d" % c, align_bytes=64)
 

@@ -47,9 +47,9 @@ def tile_picked_wpna_none_l_kernel(
         for t in range(PACK):
             nc.gpsimd.memset(h[t][:, T:WHOLE], 0.0)
 
-        def load_x(z):
-            words = x_words[z].rearrange("p n t -> p (n t)")
-            nc.sync.dma_start(x_codes[z][:].bitcast(I32), words.bitcast(I32))
+        def load_x(z, c0, c1):
+            words = x_words[z].rearrange("p n t -> p (n t)").bitcast(I32)
+            nc.sync.dma_start(x_codes[z][:, c0:c1].bitcast(I32), words[:, c0:c1])
 
         def load_w1(z, c0, c1):
             raw = keep.tile([P, PACK, c1 - c0], F32, name="w1_raw%d_%d" % (z, c0))
@@ -61,9 +61,11 @@ def tile_picked_wpna_none_l_kernel(
         w1_raw[0, 0] = load_w1(0, 0, 512)
         for q in range(4):
             nc.sync.dma_start(packed[32 * q : 32 * q + 8, :].bitcast(I32), x_scales[:, 4 * q : 4 * q + 4, :].bitcast(I32))
-        w1_raw[1, 0] = load_w1(1, 0, 512)
-        load_x(0)
-        load_x(1)
+        w1_raw[1, 0] = load_w1(1, 0, 256)
+        w1_raw[1, 256] = load_w1(1, 256, 512)
+        load_x(0, 0, T)
+        load_x(1, 0, HALF)
+        load_x(1, HALF, T)
         for d, pos in enumerate((pos1, pos2, pos3, pos4)):
             nc.sync.dma_start(lists[d][:], pos)
         w_raw = []
@@ -80,9 +82,9 @@ def tile_picked_wpna_none_l_kernel(
         w1_plane1 = keep.tile([P, T], U8, name="w1_plane1", align_bytes=64)
         w1_plane = [packed[8:P, :], w1_plane1[:]]
 
-        def cast_w1(z):
-            src = w1_raw[z, 0][:].rearrange("p j (m t) -> p m j t", t=PACK)
-            dst = w1_bf[z][:].rearrange("p t m j -> p m j t")
+        def cast_w1(z, c0, c1):
+            src = w1_raw[z, c0][:].rearrange("p j (m t) -> p m j t", t=PACK)
+            dst = w1_bf[z][:, :, c0 // PACK : c1 // PACK].rearrange("p t m j -> p m j t")
             nc.vector.tensor_copy(dst[:, :, :, 0:2], src[:, :, :, 0:2])
             nc.scalar.activation(dst[:, :, :, 2:4], src[:, :, :, 2:4], COPY)
 
@@ -93,9 +95,10 @@ def tile_picked_wpna_none_l_kernel(
                 in_=w1_bf[z][:, t0:t1].rearrange("p t m j -> p (t m j)"),
             )
 
-        cast_w1(0)
+        cast_w1(0, 0, 512)
         quantize_w1(0, 0, 4)
-        cast_w1(1)
+        cast_w1(1, 0, 256)
+        cast_w1(1, 256, 512)
         quantize_w1(1, 0, 1)
         quantize_w1(1, 1, 2)
         quantize_w1(1, 2, 4)
@@ -153,10 +156,11 @@ def tile_picked_wpna_none_l_kernel(
         def flat(tile, v0, v1):
             return tile[:, v0:v1].rearrange("p v t -> p (v t)")
 
-        mean = keep.tile([P, T, PACK], BF16, name="mean", align_bytes=64)
+        mean = {}
 
-        def finish_mean(v0, v1, b_back):
+        def turn_mean(v0, v1, b_back):
             blocks = (v1 - v0) // P
+            mean[v0] = keep.tile([P, v1 - v0, PACK], BF16, name="mean%d" % v0, tag="mean%d" % v0, align_bytes=64)
             back = bank(b_back, [P, blocks, 2, P])
             for i in range(blocks):
                 b = v0 // P + i
@@ -167,8 +171,12 @@ def tile_picked_wpna_none_l_kernel(
                 words = turned[:].rearrange("v u p e -> v u (p e)").bitcast(F32)
                 for u in range(2):
                     nc.tensor.transpose(back[:, i, u, :], words[:, u, :], identity[:])
+            return back
+
+        def finish_mean(v0, back):
+            blocks = back.shape[1]
             nc.scalar.copy(
-                mean[:, v0:v1].bitcast(F32).rearrange("p (b v) u -> p b v u", b=blocks),
+                mean[v0][:].bitcast(F32).rearrange("p (b v) u -> p b v u", b=blocks),
                 back[:].rearrange("p b u v -> p b v u"),
             )
 
@@ -195,10 +203,11 @@ def tile_picked_wpna_none_l_kernel(
                     both[:, u].rearrange("p v e -> p e v"), first[:, 2 * u : 2 * u + 2], part[:, 2 * u : 2 * u + 2], op
                 )
 
-        early = keep.tile([P, 2, T], F32, name="early", tag="held")
+        early = [keep.tile([P, T], F32, name="early0", tag="reuse1", align_bytes=64), keep.tile([P, T], F32, name="early1")]
         for t in range(2):
             gather_first(t)
-            gather_gap(t, early[:, t, :])
+        for t in range(2):
+            gather_gap(t, early[t][:])
         first_level(0)
         for t in range(2, PACK):
             gather_first(t)
@@ -214,7 +223,7 @@ def tile_picked_wpna_none_l_kernel(
 
         for d in (3,):
             rounded[d] = keep.tile([P, T, PACK], BF16, name="rounded%d" % d, align_bytes=64)
-        middle = keep.tile([P, PACK + 2, T], F32, name="middle", tag="held")
+        middle = keep.tile([P, PACK + 2, T], F32, name="middle", tag="reuse1", align_bytes=64)
         third = gather(2, middle[:, 0:PACK, :], 0, T)
         paired = keep.tile([P, 2, T, 2], BF16, name="paired")
         for u in range(2):
@@ -233,10 +242,23 @@ def tile_picked_wpna_none_l_kernel(
             )
         last = keep.tile([P, PACK, T], F32, name="last", tag="reuse0", align_bytes=64)
         round_picked(3, gather(3, last[:, :, 0:HALF], 0, HALF), 0, HALF)
-        finish_mean(0, 256, 1)
+        lower = turn_mean(0, HALF, 1)
         round_picked(3, gather(3, last[:, :, HALF:T], HALF, T), HALF, T, HALF)
-        finish_mean(256, 384, 0)
-        finish_mean(384, 512, 4)
+        finish_mean(0, lower)
+        warm = bank(1, [P, T])
+        for i in range(3):
+            nc.tensor.matmul_mx(
+                warm[:],
+                lhsT=w_codes[:, i * P : (i + 1) * P].bitcast(FP8X4),
+                lhsT_scale=w_plane[:, i * P : (i + 1) * P],
+                rhs=w_codes[:, 0:T].bitcast(FP8X4),
+                rhs_scale=w_plane[:, 0:T],
+                start=True,
+                stop=True,
+            )
+        backs = [turn_mean(256, 384, 0), turn_mean(384, 512, 4)]
+        finish_mean(256, backs[0])
+        finish_mean(384, backs[1])
 
         running = {}
         for name, op in (("max", MAX), ("min", MIN)):
@@ -246,7 +268,7 @@ def tile_picked_wpna_none_l_kernel(
             for op, both in ((MAX, max01), (MIN, min01)):
                 nc.vector.tensor_tensor(running[op][:, :, v0:v1], both[:, :, v0:v1], paired[:, :, v0:v1], op)
 
-        out_banks = ((2, 3), (5, 1), (6, 0))
+        out_banks = ((6, 7), (2, 3), (5, 1))
         for c, (v0, v1) in enumerate(PIECES):
             width = v1 - v0
             final = c == len(PIECES) - 1
@@ -270,7 +292,7 @@ def tile_picked_wpna_none_l_kernel(
                     in_=values,
                 )
 
-            quantize_z(0, 1, flat(mean, v0, v1))
+            quantize_z(0, 1, flat(mean[v0], 0, width))
             if final:
                 quantize_z(1, 2, extremes[:, 0])
                 quantize_z(2, 3, extremes[:, 1])

@@ -14,19 +14,25 @@ U16 = mybir.dt.uint16
 U8 = mybir.dt.uint8
 FP8X4 = mybir.dt.float8_e4m3fn_x4
 COPY = mybir.ActivationFunctionType.Copy
+RELU = mybir.ActivationFunctionType.Relu
 MAX = mybir.AluOpType.max
 MIN = mybir.AluOpType.min
 ADD = mybir.AluOpType.add
 SUBTRACT = mybir.AluOpType.subtract
-RELU = mybir.ActivationFunctionType.Relu
 
 P = 128
 PACK = 4
+K_PASS = P * PACK
 D = 4
-WINDOW = 704
-WHOLE = 1024
-HALF = 256
+STATS = 3
+LIST_ROWS = 16
+HALF = T // 2
+PLANE_TILE = 2 * T
+PLAIN_WINDOW = 704
 PIECES = ((0, 256), (256, 384), (384, 512))
+SUM_BANK = 4
+MEAN_BANKS = (1, 0, 4)
+OUT_BANKS = ((6, 7), (2, 3), (5, 1))
 
 
 def tile_picked_wpna_none_l_kernel(
@@ -40,12 +46,12 @@ def tile_picked_wpna_none_l_kernel(
         def bank(b, shape):
             return psum.tile(shape, F32, name="bank%d" % b, tag="bank%d" % b)
 
-        lists = [keep.tile([P, T // 16], U16, name="list%d" % d) for d in range(D)]
+        lists = [keep.tile([P, T // LIST_ROWS], U16, name="list%d" % d) for d in range(D)]
         x_codes = [keep.tile([P, T], U32, name="x_codes%d" % z, align_bytes=64) for z in range(2)]
         packed = keep.tile([P, T], U8, name="packed", align_bytes=64)
-        h = [keep.tile([P, WHOLE], F32, name="h%d" % t) for t in range(PACK)]
+        h = [keep.tile([P, PLANE_TILE], F32, name="h%d" % t) for t in range(PACK)]
         for t in range(PACK):
-            nc.gpsimd.memset(h[t][:, T:WHOLE], 0.0)
+            nc.gpsimd.memset(h[t][:, T:PLANE_TILE], 0.0)
 
         def load_x(z, c0, c1):
             words = x_words[z].rearrange("p n t -> p (n t)").bitcast(I32)
@@ -53,16 +59,15 @@ def tile_picked_wpna_none_l_kernel(
 
         def load_w1(z, c0, c1):
             raw = keep.tile([P, PACK, c1 - c0], F32, name="w1_raw%d_%d" % (z, c0))
-            rows = w1[512 * z : 512 * (z + 1), :].rearrange("(p j) c -> p j c", j=PACK)
+            rows = w1[K_PASS * z : K_PASS * (z + 1), :].rearrange("(p j) c -> p j c", j=PACK)
             nc.sync.dma_start(raw[:], rows[:, :, c0:c1])
             return raw
 
-        w1_raw = {}
-        w1_raw[0, 0] = load_w1(0, 0, 512)
+        w1_raw = {(0, 0): load_w1(0, 0, H)}
         for q in range(4):
             nc.sync.dma_start(packed[32 * q : 32 * q + 8, :].bitcast(I32), x_scales[:, 4 * q : 4 * q + 4, :].bitcast(I32))
-        w1_raw[1, 0] = load_w1(1, 0, 256)
-        w1_raw[1, 256] = load_w1(1, 256, 512)
+        w1_raw[1, 0] = load_w1(1, 0, H // 2)
+        w1_raw[1, H // 2] = load_w1(1, H // 2, H)
         load_x(0, 0, T)
         load_x(1, 0, HALF)
         load_x(1, HALF, T)
@@ -78,11 +83,11 @@ def tile_picked_wpna_none_l_kernel(
         make_identity(nc, identity[:])
 
         w1_bf = [keep.tile([P, PACK, P, PACK], BF16, name="w1_bf%d" % z, align_bytes=64) for z in range(2)]
-        w1_codes = [keep.tile([P, PACK, P], U32, name="w1_codes%d" % z, tag="reuse%d" % z, align_bytes=64) for z in range(2)]
-        w1_plane1 = keep.tile([P, T], U8, name="w1_plane1", align_bytes=64)
-        w1_plane = [packed[8:P, :], w1_plane1[:]]
+        w1_codes = [keep.tile([P, PACK, P], U32, name="w1_codes%d" % z, tag="chain%d" % z, align_bytes=64) for z in range(2)]
+        w1_scales1 = keep.tile([P, H], U8, name="w1_scales1", align_bytes=64)
+        w1_scales = [packed[8:P, :], w1_scales1[:]]
 
-        def cast_w1(z, c0, c1):
+        def round_w1(z, c0, c1):
             src = w1_raw[z, c0][:].rearrange("p j (m t) -> p m j t", t=PACK)
             dst = w1_bf[z][:, :, c0 // PACK : c1 // PACK].rearrange("p t m j -> p m j t")
             nc.vector.tensor_copy(dst[:, :, :, 0:2], src[:, :, :, 0:2])
@@ -91,48 +96,61 @@ def tile_picked_wpna_none_l_kernel(
         def quantize_w1(z, t0, t1):
             nc.vector.quantize_mx(
                 out=w1_codes[z][:, t0:t1, :].rearrange("p t m -> p (t m)").bitcast(FP8X4),
-                scales=w1_plane[z][:, t0 * P : t1 * P],
+                scales=w1_scales[z][:, t0 * P : t1 * P],
                 in_=w1_bf[z][:, t0:t1].rearrange("p t m j -> p (t m j)"),
             )
 
-        cast_w1(0, 0, 512)
-        quantize_w1(0, 0, 4)
-        cast_w1(1, 0, 256)
-        cast_w1(1, 256, 512)
+        def warm_up(b, codes, scales, passes):
+            unread = bank(b, [P, T])
+            for c0, width in passes:
+                nc.tensor.matmul_mx(
+                    unread[:, 0:width],
+                    lhsT=codes[:, c0 : c0 + P].bitcast(FP8X4),
+                    lhsT_scale=scales[:, c0 : c0 + P],
+                    rhs=codes[:, 0:width].bitcast(FP8X4),
+                    rhs_scale=scales[:, 0:width],
+                    start=True,
+                    stop=True,
+                )
+
+        round_w1(0, 0, H)
+        quantize_w1(0, 0, PACK)
+        warm_up(3, w1_codes[0][:].rearrange("p t m -> p (t m)"), w1_scales[0], ((0, T), (0, HALF)))
+        round_w1(1, 0, H // 2)
+        round_w1(1, H // 2, H)
         quantize_w1(1, 0, 1)
         quantize_w1(1, 1, 2)
-        quantize_w1(1, 2, 4)
+        quantize_w1(1, 2, PACK)
 
         def first_pass(acc, z, t, c0, c1, start):
             nc.tensor.matmul_mx(
                 acc[:],
                 lhsT=w1_codes[z][:, t, :].bitcast(FP8X4),
-                lhsT_scale=w1_plane[z][:, t * P : (t + 1) * P],
+                lhsT_scale=w1_scales[z][:, t * P : (t + 1) * P],
                 rhs=x_codes[z][:, c0:c1].bitcast(FP8X4),
                 rhs_scale=packed[4 * z : P, c0:c1],
                 start=start,
                 stop=not start,
             )
 
-        halves = [bank(b, [P, T // 2]) for b in range(2)]
+        halves = [bank(b, [P, HALF]) for b in range(2)]
         for z in range(2):
             for b in range(2):
-                first_pass(halves[b], z, 0, b * T // 2, (b + 1) * T // 2, z == 0)
-        nc.scalar.copy(h[0][:, 0 : T // 2], halves[0][:])
-        nc.vector.tensor_copy(h[0][:, T // 2 : T], halves[1][:])
+                first_pass(halves[b], z, 0, b * HALF, (b + 1) * HALF, z == 0)
+        nc.scalar.copy(h[0][:, 0:HALF], halves[0][:])
+        nc.vector.tensor_copy(h[0][:, HALF:T], halves[1][:])
         for t in range(1, PACK):
             acc = bank((1 + t) % 3, [P, T])
             first_pass(acc, 1, t, 0, T, True)
             first_pass(acc, 0, t, 0, T, False)
             nc.scalar.copy(h[t][:, 0:T], acc[:])
 
-        totals = [bank(4 + b, [P, PACK, P]) for b in range(T // P)]
-        rounded = {}
+        sums = [bank(SUM_BANK + b, [P, PACK, P]) for b in range(T // P)]
 
-        def add_turned(values, t, v0, v1, start=False, stop=False):
+        def add_to_sums(values, t, v0, v1, start=False, stop=False):
             for b in range(v0 // P, v1 // P):
                 nc.tensor.matmul(
-                    totals[b][:, t, :],
+                    sums[b][:, t, :],
                     lhsT=values[:, b * P - v0 : (b + 1) * P - v0],
                     rhs=identity[:],
                     is_transpose=True,
@@ -140,176 +158,159 @@ def tile_picked_wpna_none_l_kernel(
                     stop=stop,
                 )
 
-        def gather(d, g, v0, v1):
-            offsets = lists[d][:, v0 // 16 : v1 // 16]
+        def gather_planes(d, picked, v0, v1):
+            offsets = lists[d][:, v0 // LIST_ROWS : v1 // LIST_ROWS]
             for t in range(PACK):
-                nc.vector.tensor_copy(g[:, t, :], h[t][:, 0:WINDOW].indirect(offsets))
-                add_turned(g[:, t, :], t, v0, v1, stop=(d == D - 1 and t == PACK - 1))
-            return g
+                nc.vector.tensor_copy(picked[:, t, :], h[t][:, 0:PLAIN_WINDOW].indirect(offsets))
+                add_to_sums(picked[:, t, :], t, v0, v1, stop=(d == D - 1 and t == PACK - 1))
 
-        def round_picked(d, g, v0, v1, first=0):
-            nc.scalar.copy(
-                rounded[d][:, v0:v1].rearrange("p (c i) t -> p c t i", i=4),
-                g[:, :, v0 - first : v1 - first].rearrange("p t (c i) -> p c t i", i=4),
-            )
+        means = []
 
-        def flat(tile, v0, v1):
-            return tile[:, v0:v1].rearrange("p v t -> p (v t)")
-
-        mean = {}
-
-        def turn_mean(v0, v1, b_back):
+        def turn_mean(c):
+            v0, v1 = PIECES[c]
             blocks = (v1 - v0) // P
-            mean[v0] = keep.tile([P, v1 - v0, PACK], BF16, name="mean%d" % v0, tag="mean%d" % v0, align_bytes=64)
-            back = bank(b_back, [P, blocks, 2, P])
+            means.append(keep.tile([P, v1 - v0, PACK], BF16, name="mean%d" % c, align_bytes=64))
+            back = bank(MEAN_BANKS[c], [P, blocks, 2, P])
             for i in range(blocks):
                 b = v0 // P + i
                 turned = keep.tile([P, 2, P, 2], BF16, name="turned%d" % b)
                 nc.scalar.activation(
-                    turned[:], totals[b][:].rearrange("v (u e) p -> v u p e", e=2), COPY, scale=1.0 / D
+                    turned[:], sums[b][:].rearrange("v (u e) p -> v u p e", e=2), COPY, scale=1.0 / D
                 )
                 words = turned[:].rearrange("v u p e -> v u (p e)").bitcast(F32)
                 for u in range(2):
                     nc.tensor.transpose(back[:, i, u, :], words[:, u, :], identity[:])
             return back
 
-        def finish_mean(v0, back):
-            blocks = back.shape[1]
+        def finish_mean(c, back):
             nc.scalar.copy(
-                mean[v0][:].bitcast(F32).rearrange("p (b v) u -> p b v u", b=blocks),
+                means[c][:].bitcast(F32).rearrange("p (b v) u -> p b v u", v=P),
                 back[:].rearrange("p b u v -> p b v u"),
             )
 
-        first = keep.tile([P, PACK, T], F32, name="first")
+        a = keep.tile([P, PACK, T], F32, name="a")
         above = keep.tile([P, PACK, T], F32, name="above")
         below = keep.tile([P, PACK, T], F32, name="below")
-        max01 = keep.tile([P, 2, T, 2], BF16, name="max01")
-        min01 = keep.tile([P, 2, T, 2], BF16, name="min01")
+        max_ab = keep.tile([P, 2, T, 2], BF16, name="max_ab")
+        min_ab = keep.tile([P, 2, T, 2], BF16, name="min_ab")
 
-        def gather_first(t):
-            nc.vector.tensor_copy(first[:, t, :], h[t][:, 0:WINDOW].indirect(lists[0][:]))
-            add_turned(first[:, t, :], t, 0, T, start=(t == 0))
-            add_turned(first[:, t, :], t, 0, T)
+        def gather_a(t):
+            nc.vector.tensor_copy(a[:, t, :], h[t][:, 0:PLAIN_WINDOW].indirect(lists[0][:]))
+            add_to_sums(a[:, t, :], t, 0, T, start=(t == 0))
+            add_to_sums(a[:, t, :], t, 0, T)
 
         def gather_gap(t, gap):
-            nc.vector.tensor_tensor(gap, h[t][:].indirect(lists[1][:]), first[:, t, :], SUBTRACT)
-            add_turned(gap, t, 0, T)
+            nc.vector.tensor_tensor(gap, h[t][:].indirect(lists[1][:]), a[:, t, :], SUBTRACT)
+            add_to_sums(gap, t, 0, T)
             nc.scalar.activation(above[:, t, :], gap, RELU)
             nc.scalar.activation(below[:, t, :], gap, RELU, scale=-1.0)
 
-        def first_level(u):
-            for both, part, op in ((max01, above, ADD), (min01, below, SUBTRACT)):
+        def extremes_ab(u):
+            for result, part, op in ((max_ab, above, ADD), (min_ab, below, SUBTRACT)):
                 nc.gpsimd.tensor_tensor(
-                    both[:, u].rearrange("p v e -> p e v"), first[:, 2 * u : 2 * u + 2], part[:, 2 * u : 2 * u + 2], op
+                    result[:, u].rearrange("p v e -> p e v"), a[:, 2 * u : 2 * u + 2], part[:, 2 * u : 2 * u + 2], op
                 )
 
-        early = [keep.tile([P, T], F32, name="early0", tag="reuse1", align_bytes=64), keep.tile([P, T], F32, name="early1")]
+        gaps = [keep.tile([P, T], F32, name="gap0", tag="chain1", align_bytes=64), keep.tile([P, T], F32, name="gap1")]
         for t in range(2):
-            gather_first(t)
+            gather_a(t)
         for t in range(2):
-            gather_gap(t, early[t][:])
-        first_level(0)
+            gather_gap(t, gaps[t][:])
+        extremes_ab(0)
         for t in range(2, PACK):
-            gather_first(t)
+            gather_a(t)
 
-        w_bf = keep.tile([P, 3, N, PACK], BF16, name="w_bf", tag="reuse0", align_bytes=64)
-        w_codes = keep.tile([P, 3 * N], U32, name="w_codes", align_bytes=64)
-        w_plane = keep.tile([P, 3 * N], U8, name="w_plane", align_bytes=64)
-        for s in range(3):
+        w_bf = keep.tile([P, STATS, N, PACK], BF16, name="w_bf", tag="chain0", align_bytes=64)
+        w_codes = keep.tile([P, STATS * N], U32, name="w_codes", align_bytes=64)
+        w_scales = keep.tile([P, STATS * N], U8, name="w_scales", align_bytes=64)
+        for s in range(STATS):
             nc.scalar.copy(
                 w_bf[:, s].rearrange("p (c i) j -> p c j i", i=4),
                 w_raw[s][:].rearrange("p j (c i) -> p c j i", i=4),
             )
 
-        for d in (3,):
-            rounded[d] = keep.tile([P, T, PACK], BF16, name="rounded%d" % d, align_bytes=64)
-        middle = keep.tile([P, PACK + 2, T], F32, name="middle", tag="reuse1", align_bytes=64)
-        third = gather(2, middle[:, 0:PACK, :], 0, T)
-        paired = keep.tile([P, 2, T, 2], BF16, name="paired")
+        d_rounded = keep.tile([P, T, PACK], BF16, name="d_rounded", align_bytes=64)
+        c_and_gaps = keep.tile([P, PACK + 2, T], F32, name="c_and_gaps", tag="chain1", align_bytes=64)
+        gather_planes(2, c_and_gaps[:, 0:PACK, :], 0, T)
+        c_rounded = keep.tile([P, 2, T, 2], BF16, name="c_rounded")
         for u in range(2):
             nc.scalar.copy(
-                paired[:, u].rearrange("p (c i) e -> p c e i", i=4),
-                third[:, 2 * u : 2 * u + 2].rearrange("p e (c i) -> p c e i", i=4),
+                c_rounded[:, u].rearrange("p (c i) e -> p c e i", i=4),
+                c_and_gaps[:, 2 * u : 2 * u + 2].rearrange("p e (c i) -> p c e i", i=4),
             )
         for t in range(2, PACK):
-            gather_gap(t, middle[:, PACK + t - 2, :])
-        first_level(1)
+            gather_gap(t, c_and_gaps[:, PACK + t - 2, :])
+        extremes_ab(1)
         for s0, s1 in ((2, 3), (0, 2)):
             nc.vector.quantize_mx(
                 out=w_codes[:, s0 * N : s1 * N].bitcast(FP8X4),
-                scales=w_plane[:, s0 * N : s1 * N],
+                scales=w_scales[:, s0 * N : s1 * N],
                 in_=w_bf[:, s0:s1].rearrange("p s n j -> p (s n j)"),
             )
-        last = keep.tile([P, PACK, T], F32, name="last", tag="reuse0", align_bytes=64)
-        round_picked(3, gather(3, last[:, :, 0:HALF], 0, HALF), 0, HALF)
-        lower = turn_mean(0, HALF, 1)
-        round_picked(3, gather(3, last[:, :, HALF:T], HALF, T), HALF, T, HALF)
-        finish_mean(0, lower)
-        warm = bank(1, [P, T])
-        for i in range(3):
-            nc.tensor.matmul_mx(
-                warm[:],
-                lhsT=w_codes[:, i * P : (i + 1) * P].bitcast(FP8X4),
-                lhsT_scale=w_plane[:, i * P : (i + 1) * P],
-                rhs=w_codes[:, 0:T].bitcast(FP8X4),
-                rhs_scale=w_plane[:, 0:T],
-                start=True,
-                stop=True,
+
+        d_picked = keep.tile([P, PACK, T], F32, name="d_picked", tag="chain0", align_bytes=64)
+
+        def gather_d(v0, v1):
+            gather_planes(D - 1, d_picked[:, :, v0:v1], v0, v1)
+            nc.scalar.copy(
+                d_rounded[:, v0:v1].rearrange("p (c i) t -> p c t i", i=4),
+                d_picked[:, :, v0:v1].rearrange("p t (c i) -> p c t i", i=4),
             )
-        backs = [turn_mean(256, 384, 0), turn_mean(384, 512, 4)]
-        finish_mean(256, backs[0])
-        finish_mean(384, backs[1])
 
-        running = {}
-        for name, op in (("max", MAX), ("min", MIN)):
-            running[op] = keep.tile([P, 2, T, 2], BF16, name="%s012" % name)
+        gather_d(0, HALF)
+        back = turn_mean(0)
+        gather_d(HALF, T)
+        finish_mean(0, back)
+        warm_up(MEAN_BANKS[0], w_codes, w_scales, ((0, T), (P, T)))
+        backs = {c: turn_mean(c) for c in (1, 2)}
+        for c in (1, 2):
+            finish_mean(c, backs[c])
 
-        def second_level(v0, v1):
-            for op, both in ((MAX, max01), (MIN, min01)):
-                nc.vector.tensor_tensor(running[op][:, :, v0:v1], both[:, :, v0:v1], paired[:, :, v0:v1], op)
-
-        out_banks = ((6, 7), (2, 3), (5, 1))
+        max_abc = keep.tile([P, 2, T, 2], BF16, name="max_abc")
+        min_abc = keep.tile([P, 2, T, 2], BF16, name="min_abc")
         for c, (v0, v1) in enumerate(PIECES):
             width = v1 - v0
             final = c == len(PIECES) - 1
             if v0 % HALF == 0:
-                second_level(v0, v0 + HALF)
+                half = slice(v0, v0 + HALF)
+                for op, ab, abc in ((MAX, max_ab, max_abc), (MIN, min_ab, min_abc)):
+                    nc.vector.tensor_tensor(abc[:, :, half], ab[:, :, half], c_rounded[:, :, half], op)
             extremes = keep.tile([P, 2, width * PACK], BF16, name="extremes%d" % c, align_bytes=64)
-            for s, op in enumerate((MAX, MIN)):
+            for s, (op, abc) in enumerate(((MAX, max_abc), (MIN, min_abc))):
                 nc.vector.tensor_tensor(
                     extremes[:, s].rearrange("p (v u e) -> p v u e", u=2, e=2),
-                    running[op][:, :, v0:v1].rearrange("p u v e -> p v u e"),
-                    rounded[D - 1][:, v0:v1].rearrange("p v (u e) -> p v u e", e=2),
+                    abc[:, :, v0:v1].rearrange("p u v e -> p v u e"),
+                    d_rounded[:, v0:v1].rearrange("p v (u e) -> p v u e", e=2),
                     op,
                 )
-            codes = keep.tile([P, 3 * width], U32, name="z_codes%d" % c, align_bytes=64)
-            plane = keep.tile([P, 3 * width], U8, name="z_plane%d" % c, align_bytes=64)
+            z_codes = keep.tile([P, STATS * width], U32, name="z_codes%d" % c, align_bytes=64)
+            z_scales = keep.tile([P, STATS * width], U8, name="z_scales%d" % c, align_bytes=64)
 
             def quantize_z(s0, s1, values):
                 nc.vector.quantize_mx(
-                    out=codes[:, s0 * width : s1 * width].bitcast(FP8X4),
-                    scales=plane[:, s0 * width : s1 * width],
+                    out=z_codes[:, s0 * width : s1 * width].bitcast(FP8X4),
+                    scales=z_scales[:, s0 * width : s1 * width],
                     in_=values,
                 )
 
-            quantize_z(0, 1, flat(mean[v0], 0, width))
+            quantize_z(0, 1, means[c][:].rearrange("p v t -> p (v t)"))
             if final:
                 quantize_z(1, 2, extremes[:, 0])
                 quantize_z(2, 3, extremes[:, 1])
             else:
                 quantize_z(1, 3, extremes[:].rearrange("p s w -> p (s w)"))
-            acc = [bank(out_banks[c][m], [P, width]) for m in range(2)]
-            for s in range(3):
+            acc = [bank(OUT_BANKS[c][m], [P, width]) for m in range(2)]
+            for s in range(STATS):
                 for m in range(2):
                     cols = slice(s * N + m * P, s * N + (m + 1) * P)
                     nc.tensor.matmul_mx(
                         acc[m][:],
                         lhsT=w_codes[:, cols].bitcast(FP8X4),
-                        lhsT_scale=w_plane[:, cols],
-                        rhs=codes[:, s * width : (s + 1) * width].bitcast(FP8X4),
-                        rhs_scale=plane[:, s * width : (s + 1) * width],
+                        lhsT_scale=w_scales[:, cols],
+                        rhs=z_codes[:, s * width : (s + 1) * width].bitcast(FP8X4),
+                        rhs_scale=z_scales[:, s * width : (s + 1) * width],
                         start=(s == 0),
-                        stop=(s == 2),
+                        stop=(s == STATS - 1),
                     )
             for m in range(2):
                 result = keep.tile([P, width], F32, name="result%d_%d" % (c, m))

@@ -57,17 +57,15 @@ def tile_picked_wpna_none_l_kernel(
             words = x_words[z].rearrange("p n t -> p (n t)").bitcast(I32)
             nc.sync.dma_start(x_codes[z][:, c0:c1].bitcast(I32), words[:, c0:c1])
 
-        def load_w1(z, c0, c1):
-            raw = keep.tile([P, PACK, c1 - c0], F32, name="w1_raw%d_%d" % (z, c0))
-            rows = w1[K_PASS * z : K_PASS * (z + 1), :].rearrange("(p j) c -> p j c", j=PACK)
-            nc.sync.dma_start(raw[:], rows[:, :, c0:c1])
+        def load_w1(z):
+            raw = keep.tile([P, PACK, H], F32, name="w1_raw%d" % z)
+            nc.sync.dma_start(raw[:], w1[K_PASS * z : K_PASS * (z + 1), :].rearrange("(p j) c -> p j c", j=PACK))
             return raw
 
-        w1_raw = {(0, 0): load_w1(0, 0, H)}
+        w1_raw = [load_w1(0)]
         for q in range(4):
             nc.sync.dma_start(packed[32 * q : 32 * q + 8, :].bitcast(I32), x_scales[:, 4 * q : 4 * q + 4, :].bitcast(I32))
-        w1_raw[1, 0] = load_w1(1, 0, H // 2)
-        w1_raw[1, H // 2] = load_w1(1, H // 2, H)
+        w1_raw.append(load_w1(1))
         load_x(0, 0, T)
         load_x(1, 0, HALF)
         load_x(1, HALF, T)
@@ -87,9 +85,9 @@ def tile_picked_wpna_none_l_kernel(
         w1_scales1 = keep.tile([P, H], U8, name="w1_scales1", align_bytes=64)
         w1_scales = [packed[8:P, :], w1_scales1[:]]
 
-        def round_w1(z, c0, c1):
-            src = w1_raw[z, c0][:].rearrange("p j (m t) -> p m j t", t=PACK)
-            dst = w1_bf[z][:, :, c0 // PACK : c1 // PACK].rearrange("p t m j -> p m j t")
+        def round_w1(z):
+            src = w1_raw[z][:].rearrange("p j (m t) -> p m j t", t=PACK)
+            dst = w1_bf[z][:].rearrange("p t m j -> p m j t")
             nc.vector.tensor_copy(dst[:, :, :, 0:2], src[:, :, :, 0:2])
             nc.scalar.activation(dst[:, :, :, 2:4], src[:, :, :, 2:4], COPY)
 
@@ -113,11 +111,10 @@ def tile_picked_wpna_none_l_kernel(
                     stop=True,
                 )
 
-        round_w1(0, 0, H)
+        round_w1(0)
         quantize_w1(0, 0, PACK)
         warm_up(3, w1_codes[0][:].rearrange("p t m -> p (t m)"), w1_scales[0], ((0, T), (0, HALF)))
-        round_w1(1, 0, H // 2)
-        round_w1(1, H // 2, H)
+        round_w1(1)
         quantize_w1(1, 0, 1)
         quantize_w1(1, 1, 2)
         quantize_w1(1, 2, PACK)

@@ -14,11 +14,8 @@ U16 = mybir.dt.uint16
 U8 = mybir.dt.uint8
 FP8X4 = mybir.dt.float8_e4m3fn_x4
 COPY = mybir.ActivationFunctionType.Copy
-RELU = mybir.ActivationFunctionType.Relu
 MAX = mybir.AluOpType.max
 MIN = mybir.AluOpType.min
-ADD = mybir.AluOpType.add
-SUBTRACT = mybir.AluOpType.subtract
 
 P = 128
 PACK = 4
@@ -27,12 +24,12 @@ D = 4
 STATS = 3
 LIST_ROWS = 16
 HALF = T // 2
-PLANE_TILE = 2 * T
-PLAIN_WINDOW = 704
+PLANE_TILE = 704
 PIECES = ((0, 256), (256, 384), (384, 512))
 SUM_BANK = 4
-MEAN_BANKS = (1, 0, 4)
-OUT_BANKS = ((6, 7), (2, 3), (5, 1))
+MEAN_BANKS = (3, 4, 5)
+OUT_BANKS = (1, 2, 0)
+RUN = 2
 
 
 def tile_picked_wpna_none_l_kernel(
@@ -81,7 +78,7 @@ def tile_picked_wpna_none_l_kernel(
         make_identity(nc, identity[:])
 
         w1_bf = [keep.tile([P, PACK, P, PACK], BF16, name="w1_bf%d" % z, align_bytes=64) for z in range(2)]
-        w1_codes = [keep.tile([P, PACK, P], U32, name="w1_codes%d" % z, tag="chain%d" % z, align_bytes=64) for z in range(2)]
+        w1_codes = [keep.tile([P, PACK, P], U32, name="w1_codes%d" % z, align_bytes=64) for z in range(2)]
         w1_scales1 = keep.tile([P, H], U8, name="w1_scales1", align_bytes=64)
         w1_scales = [packed[8:P, :], w1_scales1[:]]
 
@@ -98,22 +95,8 @@ def tile_picked_wpna_none_l_kernel(
                 in_=w1_bf[z][:, t0:t1].rearrange("p t m j -> p (t m j)"),
             )
 
-        def warm_up(b, codes, scales, passes):
-            unread = bank(b, [P, T])
-            for c0, width in passes:
-                nc.tensor.matmul_mx(
-                    unread[:, 0:width],
-                    lhsT=codes[:, c0 : c0 + P].bitcast(FP8X4),
-                    lhsT_scale=scales[:, c0 : c0 + P],
-                    rhs=codes[:, 0:width].bitcast(FP8X4),
-                    rhs_scale=scales[:, 0:width],
-                    start=True,
-                    stop=True,
-                )
-
         round_w1(0)
         quantize_w1(0, 0, PACK)
-        warm_up(3, w1_codes[0][:].rearrange("p t m -> p (t m)"), w1_scales[0], ((0, T), (0, HALF)))
         round_w1(1)
         quantize_w1(1, 0, 1)
         quantize_w1(1, 1, 2)
@@ -136,108 +119,68 @@ def tile_picked_wpna_none_l_kernel(
                 first_pass(halves[b], z, 0, b * HALF, (b + 1) * HALF, z == 0)
         nc.scalar.copy(h[0][:, 0:HALF], halves[0][:])
         nc.vector.tensor_copy(h[0][:, HALF:T], halves[1][:])
+        planes = {}
         for t in range(1, PACK):
-            acc = bank((1 + t) % 3, [P, T])
-            first_pass(acc, 1, t, 0, T, True)
-            first_pass(acc, 0, t, 0, T, False)
-            nc.scalar.copy(h[t][:, 0:T], acc[:])
+            planes[t] = bank((1 + t) % 4, [P, T])
+            first_pass(planes[t], 0, t, 0, T, True)
+            first_pass(planes[t], 1, t, 0, T, False)
 
         sums = [bank(SUM_BANK + b, [P, PACK, P]) for b in range(T // P)]
+        picked = {(d, 0): keep.tile([P, PACK, T], F32, name="picked%d" % d) for d in range(2)}
+        for d in (2, 3):
+            for v0, v1 in PIECES:
+                picked[d, v0] = keep.tile([P, PACK, v1 - v0], F32, name="picked%d_%d" % (d, v0))
 
-        def add_to_sums(values, t, v0, v1, start=False, stop=False):
+        def gather(d, t, v0, v1):
+            window = h[t][:].indirect(lists[d][:, v0 // LIST_ROWS : v1 // LIST_ROWS])
+            values = picked[d, v0][:, t, :]
+            if d == 0:
+                nc.vector.tensor_copy(values, window)
+            else:
+                nc.scalar.activation(values, window, COPY)
+
+        def add_to_sums(d, t, v0, v1):
+            values = picked[d, v0][:, t, :]
             for b in range(v0 // P, v1 // P):
                 nc.tensor.matmul(
                     sums[b][:, t, :],
                     lhsT=values[:, b * P - v0 : (b + 1) * P - v0],
                     rhs=identity[:],
                     is_transpose=True,
-                    start=start,
-                    stop=stop,
+                    start=(d == 0 and t == 0),
+                    stop=(d == D - 1 and t == PACK - 1),
                 )
 
-        def gather_planes(d, picked, v0, v1):
-            offsets = lists[d][:, v0 // LIST_ROWS : v1 // LIST_ROWS]
-            for t in range(PACK):
-                nc.vector.tensor_copy(picked[:, t, :], h[t][:, 0:PLAIN_WINDOW].indirect(offsets))
-                add_to_sums(picked[:, t, :], t, v0, v1, stop=(d == D - 1 and t == PACK - 1))
-
-        means = []
-
-        def turn_mean(c):
-            v0, v1 = PIECES[c]
-            blocks = (v1 - v0) // P
-            means.append(keep.tile([P, v1 - v0, PACK], BF16, name="mean%d" % c, align_bytes=64))
-            back = bank(MEAN_BANKS[c], [P, blocks, 2, P])
-            for i in range(blocks):
-                b = v0 // P + i
-                turned = keep.tile([P, 2, P, 2], BF16, name="turned%d" % b)
-                nc.scalar.activation(
-                    turned[:], sums[b][:].rearrange("v (u e) p -> v u p e", e=2), COPY, scale=1.0 / D
-                )
-                words = turned[:].rearrange("v u p e -> v u (p e)").bitcast(F32)
-                for u in range(2):
-                    nc.tensor.transpose(back[:, i, u, :], words[:, u, :], identity[:])
-            return back
-
-        def finish_mean(c, back):
-            nc.scalar.copy(
-                means[c][:].bitcast(F32).rearrange("p (b v) u -> p b v u", v=P),
-                back[:].rearrange("p b u v -> p b v u"),
-            )
-
-        a = keep.tile([P, PACK, T], F32, name="a")
-        above = keep.tile([P, PACK, T], F32, name="above")
-        below = keep.tile([P, PACK, T], F32, name="below")
-        max_ab = keep.tile([P, 2, T, 2], BF16, name="max_ab")
-        min_ab = keep.tile([P, 2, T, 2], BF16, name="min_ab")
-
-        def gather_a(t):
-            nc.vector.tensor_copy(a[:, t, :], h[t][:, 0:PLAIN_WINDOW].indirect(lists[0][:]))
-            add_to_sums(a[:, t, :], t, 0, T, start=(t == 0))
-            add_to_sums(a[:, t, :], t, 0, T)
-
-        def gather_gap(t, gap):
-            nc.vector.tensor_tensor(gap, h[t][:].indirect(lists[1][:]), a[:, t, :], SUBTRACT)
-            add_to_sums(gap, t, 0, T)
-            nc.scalar.activation(above[:, t, :], gap, RELU)
-            nc.scalar.activation(below[:, t, :], gap, RELU, scale=-1.0)
-
-        def extremes_ab(u):
-            for result, part, op in ((max_ab, above, ADD), (min_ab, below, SUBTRACT)):
-                nc.gpsimd.tensor_tensor(
-                    result[:, u].rearrange("p v e -> p e v"), a[:, 2 * u : 2 * u + 2], part[:, 2 * u : 2 * u + 2], op
+        def first_level(result, d, v0, v1):
+            for s, op in enumerate((MAX, MIN)):
+                nc.vector.tensor_tensor(
+                    result[:, s].rearrange("p (c i) t -> p c t i", i=RUN),
+                    picked[d, v0][:].rearrange("p t (c i) -> p c t i", i=RUN),
+                    picked[d + 1, v0][:].rearrange("p t (c i) -> p c t i", i=RUN),
+                    op,
                 )
 
-        gaps = [keep.tile([P, T], F32, name="gap0", tag="chain1", align_bytes=64), keep.tile([P, T], F32, name="gap1")]
-        for t in range(2):
-            gather_a(t)
-        for t in range(2):
-            gather_gap(t, gaps[t][:])
-        extremes_ab(0)
-        for t in range(2, PACK):
-            gather_a(t)
+        for t in range(PACK):
+            gather(0, t, 0, T)
+            gather(1, t, 0, T)
+            if t + 1 < PACK - 1:
+                nc.vector.tensor_copy(h[t + 1][:, 0:T], planes[t + 1][:])
+            if t == 1:
+                nc.scalar.copy(h[PACK - 1][:, 0:T], planes[PACK - 1][:])
+        for t in range(PACK):
+            add_to_sums(0, t, 0, T)
+            add_to_sums(1, t, 0, T)
+        ab = keep.tile([P, 2, T, PACK], BF16, name="ab", align_bytes=64)
+        first_level(ab, 0, 0, T)
 
-        w_bf = keep.tile([P, STATS, N, PACK], BF16, name="w_bf", tag="chain0", align_bytes=64)
+        w_bf = keep.tile([P, STATS, N, PACK], BF16, name="w_bf", align_bytes=64)
         w_codes = keep.tile([P, STATS * N], U32, name="w_codes", align_bytes=64)
         w_scales = keep.tile([P, STATS * N], U8, name="w_scales", align_bytes=64)
         for s in range(STATS):
-            nc.scalar.copy(
+            nc.vector.tensor_copy(
                 w_bf[:, s].rearrange("p (c i) j -> p c j i", i=4),
                 w_raw[s][:].rearrange("p j (c i) -> p c j i", i=4),
             )
-
-        d_rounded = keep.tile([P, T, PACK], BF16, name="d_rounded", align_bytes=64)
-        c_and_gaps = keep.tile([P, PACK + 2, T], F32, name="c_and_gaps", tag="chain1", align_bytes=64)
-        gather_planes(2, c_and_gaps[:, 0:PACK, :], 0, T)
-        c_rounded = keep.tile([P, 2, T, 2], BF16, name="c_rounded")
-        for u in range(2):
-            nc.scalar.copy(
-                c_rounded[:, u].rearrange("p (c i) e -> p c e i", i=4),
-                c_and_gaps[:, 2 * u : 2 * u + 2].rearrange("p e (c i) -> p c e i", i=4),
-            )
-        for t in range(2, PACK):
-            gather_gap(t, c_and_gaps[:, PACK + t - 2, :])
-        extremes_ab(1)
         for s0, s1 in ((2, 3), (0, 2)):
             nc.vector.quantize_mx(
                 out=w_codes[:, s0 * N : s1 * N].bitcast(FP8X4),
@@ -245,79 +188,101 @@ def tile_picked_wpna_none_l_kernel(
                 in_=w_bf[:, s0:s1].rearrange("p s n j -> p (s n j)"),
             )
 
-        d_picked = keep.tile([P, PACK, T], F32, name="d_picked", tag="chain0", align_bytes=64)
+        def gather_piece(d, c):
+            for t in range(PACK):
+                gather(d, t, *PIECES[c])
+                add_to_sums(d, t, *PIECES[c])
 
-        def gather_d(v0, v1):
-            gather_planes(D - 1, d_picked[:, :, v0:v1], v0, v1)
+        stats = [
+            keep.tile([P, STATS, (v1 - v0) * PACK], BF16, name="stats%d" % c, align_bytes=64)
+            for c, (v0, v1) in enumerate(PIECES)
+        ]
+
+        def turn_mean(c):
+            v0, v1 = PIECES[c]
+            blocks = (v1 - v0) // P
+            back = bank(MEAN_BANKS[c], [P, blocks, 2, P])
+            for i in range(blocks):
+                b = v0 // P + i
+                words = keep.tile([P, 2, P], F32, name="turned%d" % b)[:]
+                nc.scalar.activation(
+                    words.bitcast(BF16).rearrange("v u (p e) -> v u p e", e=2),
+                    sums[b][:].rearrange("v (u e) p -> v u p e", e=2),
+                    COPY,
+                    scale=1.0 / D,
+                )
+                for u in range(2):
+                    nc.tensor.transpose(back[:, i, u, :], words[:, u, :], identity[:])
+            return back
+
+        def finish_mean(c, back):
             nc.scalar.copy(
-                d_rounded[:, v0:v1].rearrange("p (c i) t -> p c t i", i=4),
-                d_picked[:, :, v0:v1].rearrange("p t (c i) -> p c t i", i=4),
+                stats[c][:, 0].bitcast(F32).rearrange("p (b v u) -> p b v u", v=P, u=2),
+                back[:].rearrange("p b u v -> p b v u"),
             )
 
-        gather_d(0, HALF)
-        back = turn_mean(0)
-        gather_d(HALF, T)
-        finish_mean(0, back)
-        warm_up(MEAN_BANKS[0], w_codes, w_scales, ((0, T), (P, T)))
-        backs = {c: turn_mean(c) for c in (1, 2)}
-        for c in (1, 2):
-            finish_mean(c, backs[c])
-
-        max_abc = keep.tile([P, 2, T, 2], BF16, name="max_abc")
-        min_abc = keep.tile([P, 2, T, 2], BF16, name="min_abc")
-        for c, (v0, v1) in enumerate(PIECES):
-            width = v1 - v0
-            final = c == len(PIECES) - 1
-            if v0 % HALF == 0:
-                half = slice(v0, v0 + HALF)
-                for op, ab, abc in ((MAX, max_ab, max_abc), (MIN, min_ab, min_abc)):
-                    nc.vector.tensor_tensor(abc[:, :, half], ab[:, :, half], c_rounded[:, :, half], op)
-            extremes = keep.tile([P, 2, width * PACK], BF16, name="extremes%d" % c, align_bytes=64)
-            for s, (op, abc) in enumerate(((MAX, max_abc), (MIN, min_abc))):
+        def extremes(c):
+            v0, v1 = PIECES[c]
+            cd = keep.tile([P, 2, v1 - v0, PACK], BF16, name="cd%d" % c, align_bytes=64)
+            first_level(cd, 2, v0, v1)
+            for s, op in enumerate((MAX, MIN)):
                 nc.vector.tensor_tensor(
-                    extremes[:, s].rearrange("p (v u e) -> p v u e", u=2, e=2),
-                    abc[:, :, v0:v1].rearrange("p u v e -> p v u e"),
-                    d_rounded[:, v0:v1].rearrange("p v (u e) -> p v u e", e=2),
+                    stats[c][:, 1 + s],
+                    ab[:, s, v0:v1].rearrange("p v t -> p (v t)"),
+                    cd[:, s].rearrange("p v t -> p (v t)"),
                     op,
                 )
-            z_codes = keep.tile([P, STATS * width], U32, name="z_codes%d" % c, align_bytes=64)
-            z_scales = keep.tile([P, STATS * width], U8, name="z_scales%d" % c, align_bytes=64)
 
-            def quantize_z(s0, s1, values):
-                nc.vector.quantize_mx(
-                    out=z_codes[:, s0 * width : s1 * width].bitcast(FP8X4),
-                    scales=z_scales[:, s0 * width : s1 * width],
-                    in_=values,
-                )
+        z_codes, z_scales, acc = [], [], []
+        for c, (v0, v1) in enumerate(PIECES):
+            z_codes.append(keep.tile([P, STATS, v1 - v0], U32, name="z_codes%d" % c, align_bytes=64))
+            z_scales.append(keep.tile([P, STATS, v1 - v0], U8, name="z_scales%d" % c, align_bytes=64))
 
-            quantize_z(0, 1, means[c][:].rearrange("p v t -> p (v t)"))
-            if final:
-                quantize_z(1, 2, extremes[:, 0])
-                quantize_z(2, 3, extremes[:, 1])
-            else:
-                quantize_z(1, 3, extremes[:].rearrange("p s w -> p (s w)"))
-            acc = [bank(OUT_BANKS[c][m], [P, width]) for m in range(2)]
-            for s in range(STATS):
+        def multiply(c, s0, s1):
+            v0, v1 = PIECES[c]
+            nc.vector.quantize_mx(
+                out=z_codes[c][:, s0:s1].rearrange("p s w -> p (s w)").bitcast(FP8X4),
+                scales=z_scales[c][:, s0:s1].rearrange("p s w -> p (s w)"),
+                in_=stats[c][:, s0:s1].rearrange("p s w -> p (s w)"),
+            )
+            if s0 == 1:
+                acc.append(bank(OUT_BANKS[c], [P, 2, v1 - v0]))
+            for s in range(s0, s1):
                 for m in range(2):
                     cols = slice(s * N + m * P, s * N + (m + 1) * P)
                     nc.tensor.matmul_mx(
-                        acc[m][:],
+                        acc[c][:, m, :],
                         lhsT=w_codes[:, cols].bitcast(FP8X4),
                         lhsT_scale=w_scales[:, cols],
-                        rhs=z_codes[:, s * width : (s + 1) * width].bitcast(FP8X4),
-                        rhs_scale=z_scales[:, s * width : (s + 1) * width],
-                        start=(s == 0),
-                        stop=(s == STATS - 1),
+                        rhs=z_codes[c][:, s, :].bitcast(FP8X4),
+                        rhs_scale=z_scales[c][:, s, :],
+                        start=(s == 1 and m == 0),
+                        stop=(s == 0 and m == 1),
                     )
-            for m in range(2):
-                result = keep.tile([P, width], F32, name="result%d_%d" % (c, m))
-                rows = out[m * P : (m + 1) * P, v0:v1]
-                if final and m == 1:
-                    nc.vector.tensor_copy(result[:], acc[m][:])
-                    nc.sync.dma_start(rows, result[:])
-                elif final:
-                    nc.scalar.copy(result[:], acc[m][:])
-                    nc.scalar.dma_start(rows, result[:])
-                else:
-                    nc.scalar.copy(result[:], acc[m][:])
-                    nc.sync.dma_start(rows, result[:])
+
+        def store(c):
+            v0, v1 = PIECES[c]
+            result = keep.tile([P, 2, v1 - v0], F32, name="result%d" % c)
+            nc.scalar.copy(result[:], acc[c][:])
+            nc.sync.dma_start(out.rearrange("(m p) v -> p m v", p=P)[:, :, v0:v1], result[:])
+
+        for c in range(len(PIECES)):
+            gather_piece(2, c)
+            gather_piece(3, c)
+        extremes(0)
+        multiply(0, 1, 3)
+        back0 = turn_mean(0)
+        extremes(1)
+        multiply(1, 1, 3)
+        back1 = turn_mean(1)
+        finish_mean(0, back0)
+        back2 = turn_mean(2)
+        finish_mean(1, back1)
+        finish_mean(2, back2)
+        extremes(2)
+        multiply(0, 0, 1)
+        multiply(1, 0, 1)
+        multiply(2, 1, 3)
+        multiply(2, 0, 1)
+        for c in range(len(PIECES)):
+            store(c)

@@ -127,14 +127,15 @@ def tile_picked_wpna_none_l_kernel(
 
         sums = [bank(SUM_BANK + b, [P, PACK, P]) for b in range(T // P)]
         picked = {(d, 0): keep.tile([P, PACK, T], F32, name="picked%d" % d) for d in range(2)}
-        for d in (2, 3):
-            for v0, v1 in PIECES:
-                picked[d, v0] = keep.tile([P, PACK, v1 - v0], F32, name="picked%d_%d" % (d, v0))
+        for v0 in (0, HALF):
+            picked[2, v0] = keep.tile([P, PACK, HALF], F32, name="picked2_%d" % v0)
+        for v0, v1 in PIECES:
+            picked[3, v0] = keep.tile([P, PACK, v1 - v0], F32, name="picked3_%d" % v0)
 
         def gather(d, t, v0, v1):
             window = h[t][:].indirect(lists[d][:, v0 // LIST_ROWS : v1 // LIST_ROWS])
             values = picked[d, v0][:, t, :]
-            if d == 0:
+            if d == 0 or (d, t, v0) == (2, 0, 0):
                 nc.vector.tensor_copy(values, window)
             else:
                 nc.scalar.activation(values, window, COPY)
@@ -151,36 +152,32 @@ def tile_picked_wpna_none_l_kernel(
                     stop=(d == D - 1 and t == PACK - 1),
                 )
 
-        def first_level(result, d, v0, v1):
-            for s, op in enumerate((MAX, MIN)):
+        def first_level(result, left, right, ops=((0, MAX), (1, MIN))):
+            for s, op in ops:
                 nc.vector.tensor_tensor(
                     result[:, s].rearrange("p (c i) t -> p c t i", i=RUN),
-                    picked[d, v0][:].rearrange("p t (c i) -> p c t i", i=RUN),
-                    picked[d + 1, v0][:].rearrange("p t (c i) -> p c t i", i=RUN),
+                    left.rearrange("p t (c i) -> p c t i", i=RUN),
+                    right.rearrange("p t (c i) -> p c t i", i=RUN),
                     op,
                 )
 
         for t in range(PACK):
             gather(0, t, 0, T)
             gather(1, t, 0, T)
-            if t + 1 < PACK - 1:
+            if t + 1 < PACK:
                 nc.vector.tensor_copy(h[t + 1][:, 0:T], planes[t + 1][:])
-            if t == 1:
-                nc.scalar.copy(h[PACK - 1][:, 0:T], planes[PACK - 1][:])
+        gather(2, 0, 0, HALF)
         for t in range(PACK):
             add_to_sums(0, t, 0, T)
             add_to_sums(1, t, 0, T)
         ab = keep.tile([P, 2, T, PACK], BF16, name="ab", align_bytes=64)
-        first_level(ab, 0, 0, T)
+        first_level(ab, picked[0, 0][:], picked[1, 0][:])
 
         w_bf = keep.tile([P, STATS, N, PACK], BF16, name="w_bf", align_bytes=64)
         w_codes = keep.tile([P, STATS * N], U32, name="w_codes", align_bytes=64)
         w_scales = keep.tile([P, STATS * N], U8, name="w_scales", align_bytes=64)
         for s in range(STATS):
-            nc.vector.tensor_copy(
-                w_bf[:, s].rearrange("p (c i) j -> p c j i", i=4),
-                w_raw[s][:].rearrange("p j (c i) -> p c j i", i=4),
-            )
+            nc.gpsimd.tensor_copy(w_bf[:, s], w_raw[s][:].rearrange("p j n -> p n j"))
         for s0, s1 in ((2, 3), (0, 2)):
             nc.vector.quantize_mx(
                 out=w_codes[:, s0 * N : s1 * N].bitcast(FP8X4),
@@ -188,10 +185,10 @@ def tile_picked_wpna_none_l_kernel(
                 in_=w_bf[:, s0:s1].rearrange("p s n j -> p (s n j)"),
             )
 
-        def gather_piece(d, c):
-            for t in range(PACK):
-                gather(d, t, *PIECES[c])
-                add_to_sums(d, t, *PIECES[c])
+        def gather_planes(d, v0, v1, t0=0, t1=PACK):
+            for t in range(t0, t1):
+                gather(d, t, v0, v1)
+                add_to_sums(d, t, v0, v1)
 
         stats = [
             keep.tile([P, STATS, (v1 - v0) * PACK], BF16, name="stats%d" % c, align_bytes=64)
@@ -204,7 +201,10 @@ def tile_picked_wpna_none_l_kernel(
             back = bank(MEAN_BANKS[c], [P, blocks, 2, P])
             for i in range(blocks):
                 b = v0 // P + i
-                words = keep.tile([P, 2, P], F32, name="turned%d" % b)[:]
+                if b == 0:
+                    words = picked[D - 1, PIECES[-1][0]][:, 2:PACK, :]
+                else:
+                    words = keep.tile([P, 2, P], F32, name="turned%d" % b)[:]
                 nc.scalar.activation(
                     words.bitcast(BF16).rearrange("v u (p e) -> v u p e", e=2),
                     sums[b][:].rearrange("v (u e) p -> v u p e", e=2),
@@ -221,10 +221,18 @@ def tile_picked_wpna_none_l_kernel(
                 back[:].rearrange("p b u v -> p b v u"),
             )
 
+        cds = [
+            keep.tile([P, 2, v1 - v0, PACK], BF16, name="cd%d" % c, align_bytes=64) for c, (v0, v1) in enumerate(PIECES)
+        ]
+
+        def extremes_cd(c):
+            v0, v1 = PIECES[c]
+            half = v0 // HALF * HALF
+            first_level(cds[c], picked[2, half][:, :, v0 - half : v1 - half], picked[3, v0][:])
+
         def extremes(c):
             v0, v1 = PIECES[c]
-            cd = keep.tile([P, 2, v1 - v0, PACK], BF16, name="cd%d" % c, align_bytes=64)
-            first_level(cd, 2, v0, v1)
+            cd = cds[c]
             for s, op in enumerate((MAX, MIN)):
                 nc.vector.tensor_tensor(
                     stats[c][:, 1 + s],
@@ -263,24 +271,34 @@ def tile_picked_wpna_none_l_kernel(
         def store(c):
             v0, v1 = PIECES[c]
             result = keep.tile([P, 2, v1 - v0], F32, name="result%d" % c)
-            nc.scalar.copy(result[:], acc[c][:])
+            if c == 1:
+                nc.vector.tensor_copy(result[:], acc[c][:])
+            else:
+                nc.scalar.copy(result[:], acc[c][:])
             nc.sync.dma_start(out.rearrange("(m p) v -> p m v", p=P)[:, :, v0:v1], result[:])
 
-        for c in range(len(PIECES)):
-            gather_piece(2, c)
-            gather_piece(3, c)
+        add_to_sums(2, 0, 0, HALF)
+        gather_planes(2, 0, HALF, 1)
+        gather_planes(3, *PIECES[0])
+        gather_planes(2, HALF, T)
+        gather_planes(3, *PIECES[1])
+        gather_planes(3, *PIECES[2], 0, 2)
+        back0 = turn_mean(0)
+        gather_planes(3, *PIECES[2], 2, PACK)
+        extremes_cd(0)
         extremes(0)
         multiply(0, 1, 3)
-        back0 = turn_mean(0)
+        extremes_cd(1)
         extremes(1)
         multiply(1, 1, 3)
-        back1 = turn_mean(1)
         finish_mean(0, back0)
+        back1 = turn_mean(1)
         back2 = turn_mean(2)
         finish_mean(1, back1)
         finish_mean(2, back2)
-        extremes(2)
+        extremes_cd(2)
         multiply(0, 0, 1)
+        extremes(2)
         multiply(1, 0, 1)
         multiply(2, 1, 3)
         multiply(2, 0, 1)

@@ -28,8 +28,10 @@ PLANE_TILE = 704
 PIECES = ((0, 256), (256, 384), (384, 512))
 SUM_BANK = 4
 MEAN_BANKS = (3, 4, 5)
-OUT_BANKS = (1, 2, 0)
-RUN = 2
+OUT_BANKS = ((1,), (2,), (0, 6))
+LINE = 4
+EXTREMES = (MAX, MIN)
+TAGS = {(0, 0): "w1_bf1", (2, 0): "x0", (3, 0): "x1"}
 
 
 def tile_picked_wpna_none_l_kernel(
@@ -38,13 +40,14 @@ def tile_picked_wpna_none_l_kernel(
     nc = tc.nc
     with ExitStack() as ctx:
         keep = ctx.enter_context(tc.tile_pool(name="keep", bufs=1))
+        reused = ctx.enter_context(tc.tile_pool(name="reused", bufs=1))
         psum = ctx.enter_context(tc.psum_pool(name="psum", bufs=1))
 
         def bank(b, shape):
             return psum.tile(shape, F32, name="bank%d" % b, tag="bank%d" % b)
 
         lists = [keep.tile([P, T // LIST_ROWS], U16, name="list%d" % d) for d in range(D)]
-        x_codes = [keep.tile([P, T], U32, name="x_codes%d" % z, align_bytes=64) for z in range(2)]
+        x_codes = [keep.tile([P, T], U32, name="x_codes%d" % z, tag="x%d" % z, align_bytes=64) for z in range(2)]
         packed = keep.tile([P, T], U8, name="packed", align_bytes=64)
         h = [keep.tile([P, PLANE_TILE], F32, name="h%d" % t) for t in range(PACK)]
         for t in range(PACK):
@@ -70,14 +73,17 @@ def tile_picked_wpna_none_l_kernel(
             nc.sync.dma_start(lists[d][:], pos)
         w_raw = []
         for s, w in enumerate((w2, w3, w4)):
-            raw = keep.tile([P, PACK, N], F32, name="w_raw%d" % s)
+            if s == 2:
+                raw = reused.tile([P, PACK, N], F32, name="w_raw2", offset=4096)
+            else:
+                raw = keep.tile([P, PACK, N], F32, name="w_raw%d" % s)
             nc.sync.dma_start(raw[:], w.rearrange("(p j) n -> p j n", j=PACK))
             w_raw.append(raw)
 
         identity = keep.tile([P, P], F32, name="identity")
         make_identity(nc, identity[:])
 
-        w1_bf = [keep.tile([P, PACK, P, PACK], BF16, name="w1_bf%d" % z, align_bytes=64) for z in range(2)]
+        w1_bf = [keep.tile([P, PACK, P, PACK], BF16, name="w1_bf%d" % z, tag="w1_bf%d" % z, align_bytes=64) for z in range(2)]
         w1_codes = [keep.tile([P, PACK, P], U32, name="w1_codes%d" % z, align_bytes=64) for z in range(2)]
         w1_scales1 = keep.tile([P, H], U8, name="w1_scales1", align_bytes=64)
         w1_scales = [packed[8:P, :], w1_scales1[:]]
@@ -117,81 +123,112 @@ def tile_picked_wpna_none_l_kernel(
         for z in range(2):
             for b in range(2):
                 first_pass(halves[b], z, 0, b * HALF, (b + 1) * HALF, z == 0)
-        nc.scalar.copy(h[0][:, 0:HALF], halves[0][:])
-        nc.vector.tensor_copy(h[0][:, HALF:T], halves[1][:])
+        nc.vector.tensor_copy(h[0][:, 0:HALF], halves[0][:])
+        nc.scalar.copy(h[0][:, HALF:T], halves[1][:])
         planes = {}
         for t in range(1, PACK):
             planes[t] = bank((1 + t) % 4, [P, T])
-            first_pass(planes[t], 0, t, 0, T, True)
-            first_pass(planes[t], 1, t, 0, T, False)
+            first_pass(planes[t], 1, t, 0, T, True)
+            first_pass(planes[t], 0, t, 0, T, False)
 
         sums = [bank(SUM_BANK + b, [P, PACK, P]) for b in range(T // P)]
-        picked = {(d, 0): keep.tile([P, PACK, T], F32, name="picked%d" % d) for d in range(2)}
-        for v0 in (0, HALF):
-            picked[2, v0] = keep.tile([P, PACK, HALF], F32, name="picked2_%d" % v0)
+        picked = {
+            (d, u, 0): keep.tile([P, 2, T], F32, name="picked%d_%d" % (d, u), tag=TAGS.get((d, u), "p%d_%d" % (d, u)), align_bytes=64)
+            for d in range(D)
+            for u in range(2)
+            if d < 2 or u == 0
+        }
         for v0, v1 in PIECES:
-            picked[3, v0] = keep.tile([P, PACK, v1 - v0], F32, name="picked3_%d" % v0)
+            for d in (2, 3):
+                picked[d, 1, v0] = keep.tile([P, 2, v1 - v0], F32, name="picked%d_1_%d" % (d, v0))
+        summed = []
 
-        def gather(d, t, v0, v1):
+        def gather(engine, d, t, v0=0, v1=T):
             window = h[t][:].indirect(lists[d][:, v0 // LIST_ROWS : v1 // LIST_ROWS])
-            values = picked[d, v0][:, t, :]
-            if d == 0 or (d, t, v0) == (2, 0, 0):
+            base = v0 if (d, t // 2, v0) in picked else 0
+            values = picked[d, t // 2, base][:, t % 2, v0 - base : v1 - base]
+            if engine is nc.vector:
                 nc.vector.tensor_copy(values, window)
             else:
                 nc.scalar.activation(values, window, COPY)
-
-        def add_to_sums(d, t, v0, v1):
-            values = picked[d, v0][:, t, :]
             for b in range(v0 // P, v1 // P):
                 nc.tensor.matmul(
                     sums[b][:, t, :],
                     lhsT=values[:, b * P - v0 : (b + 1) * P - v0],
                     rhs=identity[:],
                     is_transpose=True,
-                    start=(d == 0 and t == 0),
-                    stop=(d == D - 1 and t == PACK - 1),
+                    start=(summed.count(b) == 0),
+                    stop=(summed.count(b) == D * PACK - 1),
                 )
+                summed.append(b)
 
-        def first_level(result, left, right, ops=((0, MAX), (1, MIN))):
-            for s, op in ops:
-                nc.vector.tensor_tensor(
-                    result[:, s].rearrange("p (c i) t -> p c t i", i=RUN),
-                    left.rearrange("p t (c i) -> p c t i", i=RUN),
-                    right.rearrange("p t (c i) -> p c t i", i=RUN),
-                    op,
-                )
-
-        for t in range(PACK):
-            gather(0, t, 0, T)
-            gather(1, t, 0, T)
-            if t + 1 < PACK:
-                nc.vector.tensor_copy(h[t + 1][:, 0:T], planes[t + 1][:])
-        gather(2, 0, 0, HALF)
-        for t in range(PACK):
-            add_to_sums(0, t, 0, T)
-            add_to_sums(1, t, 0, T)
-        ab = keep.tile([P, 2, T, PACK], BF16, name="ab", align_bytes=64)
-        first_level(ab, picked[0, 0][:], picked[1, 0][:])
+        def empty(t):
+            nc.vector.tensor_copy(h[t][:, 0:T], planes[t][:])
 
         w_bf = keep.tile([P, STATS, N, PACK], BF16, name="w_bf", align_bytes=64)
-        w_codes = keep.tile([P, STATS * N], U32, name="w_codes", align_bytes=64)
-        w_scales = keep.tile([P, STATS * N], U8, name="w_scales", align_bytes=64)
-        for s in range(STATS):
+        for s in range(2):
             nc.gpsimd.tensor_copy(w_bf[:, s], w_raw[s][:].rearrange("p j n -> p n j"))
-        for s0, s1 in ((2, 3), (0, 2)):
+
+        ab = reused.tile([P, 2, 2, T, 2], BF16, name="ab", offset=4096)
+
+        V, S = nc.vector, nc.scalar
+        gather(V, 0, 0)
+        gather(S, 1, 0)
+        nc.scalar.copy(h[1][:, 0:T], planes[1][:])
+        empty(2)
+        gather(V, 0, 1)
+        gather(S, 1, 1)
+        nc.gpsimd.tensor_copy(w_bf[:, 2], w_raw[2][:].rearrange("p j n -> p n j"))
+        for d in range(2):
+            nc.gpsimd.tensor_copy(ab[:, 1, d], picked[d, 0, 0][:].rearrange("p e v -> p v e"))
+        empty(3)
+        gather(V, 0, 2)
+        gather(S, 1, 2)
+        gather(V, 0, 3)
+        gather(S, 1, 3)
+        gather(S, 2, 0)
+        gather(V, 2, 1, 0, HALF)
+        gather(S, 2, 1, HALF, T)
+        gather(S, 3, 0)
+        gather(S, 3, 1)
+        for v0, v1 in PIECES:
+            for d in (2, 3):
+                for t in (2, 3):
+                    gather(S, d, t, v0, v1)
+
+        def first_level(result, d, u, s, v0=0, v1=T):
+            nc.vector.tensor_tensor(
+                result[:, u, s, v0:v1].rearrange("p (c i) e -> p c e i", i=LINE),
+                picked[d, u, v0][:].rearrange("p e (c i) -> p c e i", i=LINE),
+                picked[d + 1, u, v0][:].rearrange("p e (c i) -> p c e i", i=LINE),
+                EXTREMES[s],
+            )
+
+        def high_level(result, d, s, v0, v1):
+            first_level(result, d, 1, s, v0, v1)
+
+        for s, op in enumerate(EXTREMES):
+            nc.vector.tensor_tensor(ab[:, 0, s], ab[:, 1, 0], ab[:, 1, 1], op)
+        w_codes = keep.tile([P, STATS * N], U32, name="w_codes", tag="w1_bf1", align_bytes=64)
+        w_scales = keep.tile([P, STATS * N], U8, name="w_scales", align_bytes=64)
+        for s0, s1 in ((0, 2), (2, 3)):
             nc.vector.quantize_mx(
                 out=w_codes[:, s0 * N : s1 * N].bitcast(FP8X4),
                 scales=w_scales[:, s0 * N : s1 * N],
                 in_=w_bf[:, s0:s1].rearrange("p s n j -> p (s n j)"),
             )
+        cd = keep.tile([P, 2, 2, T, 2], BF16, name="cd", tag="p1_0", align_bytes=64)
+        for s in range(2):
+            first_level(ab, 0, 1, s)
+        for s in range(2):
+            first_level(cd, 2, 0, s)
 
-        def gather_planes(d, v0, v1, t0=0, t1=PACK):
-            for t in range(t0, t1):
-                gather(d, t, v0, v1)
-                add_to_sums(d, t, v0, v1)
-
-        stats = [
-            keep.tile([P, STATS, (v1 - v0) * PACK], BF16, name="stats%d" % c, align_bytes=64)
+        means = [
+            keep.tile([P, 1, v1 - v0, PACK], BF16, name="mean%d" % c, align_bytes=64)
+            for c, (v0, v1) in enumerate(PIECES)
+        ]
+        extreme = [
+            keep.tile([P, 2, v1 - v0, PACK], BF16, name="extreme%d" % c, tag=("turned3", "e1", "e2")[c], align_bytes=64)
             for c, (v0, v1) in enumerate(PIECES)
         ]
 
@@ -201,12 +238,9 @@ def tile_picked_wpna_none_l_kernel(
             back = bank(MEAN_BANKS[c], [P, blocks, 2, P])
             for i in range(blocks):
                 b = v0 // P + i
-                if b == 0:
-                    words = picked[D - 1, PIECES[-1][0]][:, 2:PACK, :]
-                else:
-                    words = keep.tile([P, 2, P], F32, name="turned%d" % b)[:]
+                words = keep.tile([P, 2, P], F32, name="turned%d" % b, tag="turned%d" % b, align_bytes=64)
                 nc.scalar.activation(
-                    words.bitcast(BF16).rearrange("v u (p e) -> v u p e", e=2),
+                    words[:].bitcast(BF16).rearrange("v u (p e) -> v u p e", e=2),
                     sums[b][:].rearrange("v (u e) p -> v u p e", e=2),
                     COPY,
                     scale=1.0 / D,
@@ -217,90 +251,88 @@ def tile_picked_wpna_none_l_kernel(
 
         def finish_mean(c, back):
             nc.scalar.copy(
-                stats[c][:, 0].bitcast(F32).rearrange("p (b v u) -> p b v u", v=P, u=2),
+                means[c][:, 0].bitcast(F32).rearrange("p (b v) u -> p b v u", v=P),
                 back[:].rearrange("p b u v -> p b v u"),
             )
 
-        cds = [
-            keep.tile([P, 2, v1 - v0, PACK], BF16, name="cd%d" % c, align_bytes=64) for c, (v0, v1) in enumerate(PIECES)
-        ]
-
-        def extremes_cd(c):
+        def last_level(c):
             v0, v1 = PIECES[c]
-            half = v0 // HALF * HALF
-            first_level(cds[c], picked[2, half][:, :, v0 - half : v1 - half], picked[3, v0][:])
-
-        def extremes(c):
-            v0, v1 = PIECES[c]
-            cd = cds[c]
-            for s, op in enumerate((MAX, MIN)):
+            for s, op in enumerate(EXTREMES):
                 nc.vector.tensor_tensor(
-                    stats[c][:, 1 + s],
-                    ab[:, s, v0:v1].rearrange("p v t -> p (v t)"),
-                    cd[:, s].rearrange("p v t -> p (v t)"),
+                    extreme[c][:, s].rearrange("p v (u e) -> p v u e", e=2),
+                    ab[:, :, s, v0:v1].rearrange("p u v e -> p v u e"),
+                    cd[:, :, s, v0:v1].rearrange("p u v e -> p v u e"),
                     op,
                 )
 
-        z_codes, z_scales, acc = [], [], []
+        z_codes, z_scales, acc, passes = [], [], {}, []
         for c, (v0, v1) in enumerate(PIECES):
-            z_codes.append(keep.tile([P, STATS, v1 - v0], U32, name="z_codes%d" % c, align_bytes=64))
+            z_codes.append(keep.tile([P, 2, v1 - v0], U32, name="z_codes%d" % c, align_bytes=64))
             z_scales.append(keep.tile([P, STATS, v1 - v0], U8, name="z_scales%d" % c, align_bytes=64))
 
         def multiply(c, s0, s1):
             v0, v1 = PIECES[c]
+            if s0 == 0:
+                codes = keep.tile([P, 1, v1 - v0], U32, name="mean_codes%d" % c, tag=("e1", "p1_0", "m2")[c], align_bytes=64)[:]
+            else:
+                codes = z_codes[c][:, s0 - 1 : s1 - 1]
             nc.vector.quantize_mx(
-                out=z_codes[c][:, s0:s1].rearrange("p s w -> p (s w)").bitcast(FP8X4),
+                out=codes.rearrange("p s w -> p (s w)").bitcast(FP8X4),
                 scales=z_scales[c][:, s0:s1].rearrange("p s w -> p (s w)"),
-                in_=stats[c][:, s0:s1].rearrange("p s w -> p (s w)"),
+                in_=(means[c][:] if s0 == 0 else extreme[c][:, s0 - 1 : s1 - 1]).rearrange("p s v t -> p (s v t)"),
             )
-            if s0 == 1:
-                acc.append(bank(OUT_BANKS[c], [P, 2, v1 - v0]))
+            banks = OUT_BANKS[c]
+            if c not in acc:
+                acc[c] = [bank(b, [P, 2 // len(banks), v1 - v0]) for b in banks]
             for s in range(s0, s1):
                 for m in range(2):
                     cols = slice(s * N + m * P, s * N + (m + 1) * P)
+                    group = (c, m % len(banks))
                     nc.tensor.matmul_mx(
-                        acc[c][:, m, :],
+                        acc[c][m % len(banks)][:, m // len(banks), :],
                         lhsT=w_codes[:, cols].bitcast(FP8X4),
                         lhsT_scale=w_scales[:, cols],
-                        rhs=z_codes[c][:, s, :].bitcast(FP8X4),
+                        rhs=codes[:, s - s0, :].bitcast(FP8X4),
                         rhs_scale=z_scales[c][:, s, :],
-                        start=(s == 1 and m == 0),
-                        stop=(s == 0 and m == 1),
+                        start=(passes.count(group) == 0),
+                        stop=(passes.count(group) == 2 * STATS // len(banks) - 1),
                     )
+                    passes.append(group)
 
         def store(c):
             v0, v1 = PIECES[c]
-            result = keep.tile([P, 2, v1 - v0], F32, name="result%d" % c)
-            if c == 1:
-                nc.vector.tensor_copy(result[:], acc[c][:])
+            rows = out.rearrange("(m p) v -> p m v", p=P)[:, :, v0:v1]
+            if len(acc[c]) == 1:
+                result = keep.tile([P, 2, v1 - v0], F32, name="result%d" % c)
+                nc.scalar.copy(result[:], acc[c][0][:])
+                nc.sync.dma_start(rows, result[:])
             else:
-                nc.scalar.copy(result[:], acc[c][:])
-            nc.sync.dma_start(out.rearrange("(m p) v -> p m v", p=P)[:, :, v0:v1], result[:])
+                results = [keep.tile([P, 1, v1 - v0], F32, name="result%d_%d" % (c, m)) for m in range(2)]
+                nc.scalar.copy(results[0][:], acc[c][0][:])
+                nc.scalar.dma_start(rows[:, 0:1, :], results[0][:])
+                nc.vector.tensor_copy(results[1][:], acc[c][1][:])
+                nc.sync.dma_start(rows[:, 1:2, :], results[1][:])
 
-        add_to_sums(2, 0, 0, HALF)
-        gather_planes(2, 0, HALF, 1)
-        gather_planes(3, *PIECES[0])
-        gather_planes(2, HALF, T)
-        gather_planes(3, *PIECES[1])
-        gather_planes(3, *PIECES[2], 0, 2)
-        back0 = turn_mean(0)
-        gather_planes(3, *PIECES[2], 2, PACK)
-        extremes_cd(0)
-        extremes(0)
+        backs = [turn_mean(c) for c in range(2)]
+        finish_mean(0, backs[0])
+        high_level(cd, 2, 0, *PIECES[0])
+        high_level(cd, 2, 1, *PIECES[0])
+        last_level(0)
+        high_level(cd, 2, 0, *PIECES[1])
         multiply(0, 1, 3)
-        extremes_cd(1)
-        extremes(1)
+        backs.append(turn_mean(2))
+        finish_mean(1, backs[1])
+        finish_mean(2, backs[2])
+        high_level(cd, 2, 1, *PIECES[1])
+        last_level(1)
+        high_level(cd, 2, 0, *PIECES[2])
         multiply(1, 1, 3)
-        finish_mean(0, back0)
-        back1 = turn_mean(1)
-        back2 = turn_mean(2)
-        finish_mean(1, back1)
-        finish_mean(2, back2)
-        extremes_cd(2)
+        high_level(cd, 2, 1, *PIECES[2])
         multiply(0, 0, 1)
-        extremes(2)
+        last_level(2)
         multiply(1, 0, 1)
-        multiply(2, 1, 3)
+        multiply(2, 1, 2)
         multiply(2, 0, 1)
+        multiply(2, 2, 3)
         for c in range(len(PIECES)):
             store(c)

from contextlib import ExitStack

import concourse.mybir as mybir
from concourse.masks import make_identity

K, T, H, N = 1024, 512, 512, 256
FLOPS = 2 * K * H * T + 3 * 2 * H * N * T

F32 = mybir.dt.float32
BF16 = mybir.dt.bfloat16
I32 = mybir.dt.int32
U32 = mybir.dt.uint32
U16 = mybir.dt.uint16
U8 = mybir.dt.uint8
FP8X4 = mybir.dt.float8_e4m3fn_x4
COPY = mybir.ActivationFunctionType.Copy
MAX = mybir.AluOpType.max
MIN = mybir.AluOpType.min

P = 128
PACK = 4
K_PASS = P * PACK
D = 4
STATS = 3
LIST_ROWS = 16
HALF = T // 2
PLANE_TILE = 704
PIECES = ((0, 256), (256, 384), (384, 512))
SUM_BANK = 4
MEAN_BANKS = (3, 4, 5)
OUT_BANKS = ((1,), (2,), (0, 6))
LINE = 4
EXTREMES = (MAX, MIN)
TAGS = {(0, 0): "w1_bf1", (2, 0): "x0", (3, 0): "x1"}


def tile_picked_wpna_none_l_kernel(
    tc, x_words, x_scales, w1, w2, w3, w4, pos1, pos2, pos3, pos4, out
):
    nc = tc.nc
    with ExitStack() as ctx:
        keep = ctx.enter_context(tc.tile_pool(name="keep", bufs=1))
        reused = ctx.enter_context(tc.tile_pool(name="reused", bufs=1))
        psum = ctx.enter_context(tc.psum_pool(name="psum", bufs=1))

        def bank(b, shape):
            return psum.tile(shape, F32, name="bank%d" % b, tag="bank%d" % b)

        lists = [keep.tile([P, T // LIST_ROWS], U16, name="list%d" % d) for d in range(D)]
        x_codes = [keep.tile([P, T], U32, name="x_codes%d" % z, tag="x%d" % z, align_bytes=64) for z in range(2)]
        packed = keep.tile([P, T], U8, name="packed", align_bytes=64)
        h = [keep.tile([P, PLANE_TILE], F32, name="h%d" % t) for t in range(PACK)]
        for t in range(PACK):
            nc.gpsimd.memset(h[t][:, T:PLANE_TILE], 0.0)

        def load_x(z, c0, c1):
            words = x_words[z].rearrange("p n t -> p (n t)").bitcast(I32)
            nc.sync.dma_start(x_codes[z][:, c0:c1].bitcast(I32), words[:, c0:c1])

        def load_w1(z):
            raw = keep.tile([P, PACK, H], F32, name="w1_raw%d" % z)
            nc.sync.dma_start(raw[:], w1[K_PASS * z : K_PASS * (z + 1), :].rearrange("(p j) c -> p j c", j=PACK))
            return raw

        w1_raw = [load_w1(0)]
        for q in range(4):
            nc.sync.dma_start(packed[32 * q : 32 * q + 8, :].bitcast(I32), x_scales[:, 4 * q : 4 * q + 4, :].bitcast(I32))
        w1_raw.append(load_w1(1))
        load_x(0, 0, T)
        load_x(1, 0, HALF)
        load_x(1, HALF, T)
        for d, pos in enumerate((pos1, pos2, pos3, pos4)):
            nc.sync.dma_start(lists[d][:], pos)
        w_raw = []
        for s, w in enumerate((w2, w3, w4)):
            if s == 2:
                raw = reused.tile([P, PACK, N], F32, name="w_raw2", offset=4096)
            else:
                raw = keep.tile([P, PACK, N], F32, name="w_raw%d" % s)
            nc.sync.dma_start(raw[:], w.rearrange("(p j) n -> p j n", j=PACK))
            w_raw.append(raw)

        identity = keep.tile([P, P], F32, name="identity")
        make_identity(nc, identity[:])

        w1_bf = [keep.tile([P, PACK, P, PACK], BF16, name="w1_bf%d" % z, tag="w1_bf%d" % z, align_bytes=64) for z in range(2)]
        w1_codes = [keep.tile([P, PACK, P], U32, name="w1_codes%d" % z, align_bytes=64) for z in range(2)]
        w1_scales1 = keep.tile([P, H], U8, name="w1_scales1", align_bytes=64)
        w1_scales = [packed[8:P, :], w1_scales1[:]]

        def round_w1(z):
            src = w1_raw[z][:].rearrange("p j (m t) -> p m j t", t=PACK)
            dst = w1_bf[z][:].rearrange("p t m j -> p m j t")
            nc.vector.tensor_copy(dst[:, :, :, 0:2], src[:, :, :, 0:2])
            nc.scalar.activation(dst[:, :, :, 2:4], src[:, :, :, 2:4], COPY)

        def quantize_w1(z, t0, t1):
            nc.vector.quantize_mx(
                out=w1_codes[z][:, t0:t1, :].rearrange("p t m -> p (t m)").bitcast(FP8X4),
                scales=w1_scales[z][:, t0 * P : t1 * P],
                in_=w1_bf[z][:, t0:t1].rearrange("p t m j -> p (t m j)"),
            )

        round_w1(0)
        quantize_w1(0, 0, PACK)
        round_w1(1)
        quantize_w1(1, 0, 1)
        quantize_w1(1, 1, 2)
        quantize_w1(1, 2, PACK)

        def first_pass(acc, z, t, c0, c1, start):
            nc.tensor.matmul_mx(
                acc[:],
                lhsT=w1_codes[z][:, t, :].bitcast(FP8X4),
                lhsT_scale=w1_scales[z][:, t * P : (t + 1) * P],
                rhs=x_codes[z][:, c0:c1].bitcast(FP8X4),
                rhs_scale=packed[4 * z : P, c0:c1],
                start=start,
                stop=not start,
            )

        halves = [bank(b, [P, HALF]) for b in range(2)]
        for z in range(2):
            for b in range(2):
                first_pass(halves[b], z, 0, b * HALF, (b + 1) * HALF, z == 0)
        nc.vector.tensor_copy(h[0][:, 0:HALF], halves[0][:])
        nc.scalar.copy(h[0][:, HALF:T], halves[1][:])
        planes = {}
        for t in range(1, PACK):
            planes[t] = bank((1 + t) % 4, [P, T])
            first_pass(planes[t], 1, t, 0, T, True)
            first_pass(planes[t], 0, t, 0, T, False)

        sums = [bank(SUM_BANK + b, [P, PACK, P]) for b in range(T // P)]
        picked = {
            (d, u, 0): keep.tile([P, 2, T], F32, name="picked%d_%d" % (d, u), tag=TAGS.get((d, u), "p%d_%d" % (d, u)), align_bytes=64)
            for d in range(D)
            for u in range(2)
            if d < 2 or u == 0
        }
        for v0, v1 in PIECES:
            for d in (2, 3):
                picked[d, 1, v0] = keep.tile([P, 2, v1 - v0], F32, name="picked%d_1_%d" % (d, v0))
        summed = []

        def gather(engine, d, t, v0=0, v1=T):
            window = h[t][:].indirect(lists[d][:, v0 // LIST_ROWS : v1 // LIST_ROWS])
            base = v0 if (d, t // 2, v0) in picked else 0
            values = picked[d, t // 2, base][:, t % 2, v0 - base : v1 - base]
            if engine is nc.vector:
                nc.vector.tensor_copy(values, window)
            else:
                nc.scalar.activation(values, window, COPY)
            for b in range(v0 // P, v1 // P):
                nc.tensor.matmul(
                    sums[b][:, t, :],
                    lhsT=values[:, b * P - v0 : (b + 1) * P - v0],
                    rhs=identity[:],
                    is_transpose=True,
                    start=(summed.count(b) == 0),
                    stop=(summed.count(b) == D * PACK - 1),
                )
                summed.append(b)

        def empty(t):
            nc.vector.tensor_copy(h[t][:, 0:T], planes[t][:])

        w_bf = keep.tile([P, STATS, N, PACK], BF16, name="w_bf", align_bytes=64)
        for s in range(2):
            nc.gpsimd.tensor_copy(w_bf[:, s], w_raw[s][:].rearrange("p j n -> p n j"))

        ab = reused.tile([P, 2, 2, T, 2], BF16, name="ab", offset=4096)

        V, S = nc.vector, nc.scalar
        gather(V, 0, 0)
        gather(S, 1, 0)
        nc.scalar.copy(h[1][:, 0:T], planes[1][:])
        empty(2)
        gather(V, 0, 1)
        gather(S, 1, 1)
        nc.gpsimd.tensor_copy(w_bf[:, 2], w_raw[2][:].rearrange("p j n -> p n j"))
        for d in range(2):
            nc.gpsimd.tensor_copy(ab[:, 1, d], picked[d, 0, 0][:].rearrange("p e v -> p v e"))
        empty(3)
        gather(V, 0, 2)
        gather(S, 1, 2)
        gather(V, 0, 3)
        gather(S, 1, 3)
        gather(S, 2, 0)
        gather(V, 2, 1, 0, HALF)
        gather(S, 2, 1, HALF, T)
        gather(S, 3, 0)
        gather(S, 3, 1)
        for v0, v1 in PIECES:
            for d in (2, 3):
                for t in (2, 3):
                    gather(S, d, t, v0, v1)

        def first_level(result, d, u, s, v0=0, v1=T):
            nc.vector.tensor_tensor(
                result[:, u, s, v0:v1].rearrange("p (c i) e -> p c e i", i=LINE),
                picked[d, u, v0][:].rearrange("p e (c i) -> p c e i", i=LINE),
                picked[d + 1, u, v0][:].rearrange("p e (c i) -> p c e i", i=LINE),
                EXTREMES[s],
            )

        def high_level(result, d, s, v0, v1):
            first_level(result, d, 1, s, v0, v1)

        for s, op in enumerate(EXTREMES):
            nc.vector.tensor_tensor(ab[:, 0, s], ab[:, 1, 0], ab[:, 1, 1], op)
        w_codes = keep.tile([P, STATS * N], U32, name="w_codes", tag="w1_bf1", align_bytes=64)
        w_scales = keep.tile([P, STATS * N], U8, name="w_scales", align_bytes=64)
        for s0, s1 in ((0, 2), (2, 3)):
            nc.vector.quantize_mx(
                out=w_codes[:, s0 * N : s1 * N].bitcast(FP8X4),
                scales=w_scales[:, s0 * N : s1 * N],
                in_=w_bf[:, s0:s1].rearrange("p s n j -> p (s n j)"),
            )
        cd = keep.tile([P, 2, 2, T, 2], BF16, name="cd", tag="p1_0", align_bytes=64)
        for s in range(2):
            first_level(ab, 0, 1, s)
        for s in range(2):
            first_level(cd, 2, 0, s)

        means = [
            keep.tile([P, 1, v1 - v0, PACK], BF16, name="mean%d" % c, align_bytes=64)
            for c, (v0, v1) in enumerate(PIECES)
        ]
        extreme = [
            keep.tile([P, 2, v1 - v0, PACK], BF16, name="extreme%d" % c, tag=("turned3", "e1", "e2")[c], align_bytes=64)
            for c, (v0, v1) in enumerate(PIECES)
        ]

        def turn_mean(c):
            v0, v1 = PIECES[c]
            blocks = (v1 - v0) // P
            back = bank(MEAN_BANKS[c], [P, blocks, 2, P])
            for i in range(blocks):
                b = v0 // P + i
                words = keep.tile([P, 2, P], F32, name="turned%d" % b, tag="turned%d" % b, align_bytes=64)
                nc.scalar.activation(
                    words[:].bitcast(BF16).rearrange("v u (p e) -> v u p e", e=2),
                    sums[b][:].rearrange("v (u e) p -> v u p e", e=2),
                    COPY,
                    scale=1.0 / D,
                )
                for u in range(2):
                    nc.tensor.transpose(back[:, i, u, :], words[:, u, :], identity[:])
            return back

        def finish_mean(c, back):
            nc.scalar.copy(
                means[c][:, 0].bitcast(F32).rearrange("p (b v) u -> p b v u", v=P),
                back[:].rearrange("p b u v -> p b v u"),
            )

        def last_level(c):
            v0, v1 = PIECES[c]
            for s, op in enumerate(EXTREMES):
                nc.vector.tensor_tensor(
                    extreme[c][:, s].rearrange("p v (u e) -> p v u e", e=2),
                    ab[:, :, s, v0:v1].rearrange("p u v e -> p v u e"),
                    cd[:, :, s, v0:v1].rearrange("p u v e -> p v u e"),
                    op,
                )

        z_codes, z_scales, acc, passes = [], [], {}, []
        for c, (v0, v1) in enumerate(PIECES):
            z_codes.append(keep.tile([P, 2, v1 - v0], U32, name="z_codes%d" % c, align_bytes=64))
            z_scales.append(keep.tile([P, STATS, v1 - v0], U8, name="z_scales%d" % c, align_bytes=64))

        def multiply(c, s0, s1):
            v0, v1 = PIECES[c]
            if s0 == 0:
                codes = keep.tile([P, 1, v1 - v0], U32, name="mean_codes%d" % c, tag=("e1", "p1_0", "m2")[c], align_bytes=64)[:]
            else:
                codes = z_codes[c][:, s0 - 1 : s1 - 1]
            nc.vector.quantize_mx(
                out=codes.rearrange("p s w -> p (s w)").bitcast(FP8X4),
                scales=z_scales[c][:, s0:s1].rearrange("p s w -> p (s w)"),
                in_=(means[c][:] if s0 == 0 else extreme[c][:, s0 - 1 : s1 - 1]).rearrange("p s v t -> p (s v t)"),
            )
            banks = OUT_BANKS[c]
            if c not in acc:
                acc[c] = [bank(b, [P, 2 // len(banks), v1 - v0]) for b in banks]
            for s in range(s0, s1):
                for m in range(2):
                    cols = slice(s * N + m * P, s * N + (m + 1) * P)
                    group = (c, m % len(banks))
                    nc.tensor.matmul_mx(
                        acc[c][m % len(banks)][:, m // len(banks), :],
                        lhsT=w_codes[:, cols].bitcast(FP8X4),
                        lhsT_scale=w_scales[:, cols],
                        rhs=codes[:, s - s0, :].bitcast(FP8X4),
                        rhs_scale=z_scales[c][:, s, :],
                        start=(passes.count(group) == 0),
                        stop=(passes.count(group) == 2 * STATS // len(banks) - 1),
                    )
                    passes.append(group)

        def store(c):
            v0, v1 = PIECES[c]
            rows = out.rearrange("(m p) v -> p m v", p=P)[:, :, v0:v1]
            if len(acc[c]) == 1:
                result = keep.tile([P, 2, v1 - v0], F32, name="result%d" % c)
                nc.scalar.copy(result[:], acc[c][0][:])
                nc.sync.dma_start(rows, result[:])
            else:
                results = [keep.tile([P, 1, v1 - v0], F32, name="result%d_%d" % (c, m)) for m in range(2)]
                nc.scalar.copy(results[0][:], acc[c][0][:])
                nc.scalar.dma_start(rows[:, 0:1, :], results[0][:])
                nc.vector.tensor_copy(results[1][:], acc[c][1][:])
                nc.sync.dma_start(rows[:, 1:2, :], results[1][:])

        backs = [turn_mean(c) for c in range(2)]
        finish_mean(0, backs[0])
        high_level(cd, 2, 0, *PIECES[0])
        high_level(cd, 2, 1, *PIECES[0])
        last_level(0)
        high_level(cd, 2, 0, *PIECES[1])
        multiply(0, 1, 3)
        backs.append(turn_mean(2))
        finish_mean(1, backs[1])
        finish_mean(2, backs[2])
        high_level(cd, 2, 1, *PIECES[1])
        last_level(1)
        high_level(cd, 2, 0, *PIECES[2])
        multiply(1, 1, 3)
        high_level(cd, 2, 1, *PIECES[2])
        multiply(0, 0, 1)
        last_level(2)
        multiply(1, 0, 1)
        multiply(2, 1, 2)
        multiply(2, 0, 1)
        multiply(2, 2, 3)
        for c in range(len(PIECES)):
            store(c)
